import numpy as np
import ml_dtypes


def mxq(x, axis, fmt="e4m3"):
    dtype, down = {"e4m3": (ml_dtypes.float8_e4m3fn, 7), "e5m2": (ml_dtypes.float8_e5m2, 14)}[fmt]
    v = np.moveaxis(np.asarray(x, np.float32).astype(ml_dtypes.bfloat16).astype(np.float64), axis, -1)
    blocks = v.reshape(v.shape[:-1] + (-1, 32))
    amax = np.abs(blocks).max(-1, keepdims=True)
    byte = np.maximum(np.where(amax > 0, np.frexp(amax)[1] - 1 + 127, 0) - down, 1)
    scale = np.exp2(byte - 127.0)
    codes = (blocks / scale).astype(np.float32).astype(dtype).astype(np.float64)
    return np.moveaxis((codes * scale).reshape(v.shape), -1, axis)


WIDE = False


def mx_kscale(k):
    if not WIDE:
        return np.ones(k)
    levels = np.array([10, -10, 5, -5, 0])
    if k % 512:
        return np.exp2(np.random.permutation(np.resize(levels, k // 32))).repeat(32)
    a = np.empty((k // 512, 16))
    for p in range(k // 512):
        a[p, :8] = np.random.permutation(np.resize(levels, 8))
        for g in range(8):
            far = levels[np.abs(levels - a[p, g]) >= 10]
            a[p, g + 8] = far[np.random.randint(len(far))]
    return np.exp2(a.ravel()).repeat(32)


BF16 = ml_dtypes.bfloat16


def bf(x):
    return np.asarray(x, np.float32).astype(BF16)


def f64(x):
    return np.asarray(x).astype(np.float64)


M, N, D, V = 2, 4096, 512, 512

EPS = 0.001
DELTA = 0.3
SPREAD = 0.65 * np.sqrt(2.0 * (np.log(V) - np.log(DELTA / EPS)))


def draw0():
    s, t = mx_kscale(D), mx_kscale(D)
    return {
        "h": bf(np.random.standard_normal((N, D)) * s),
        "w_res": bf(np.random.standard_normal((M, D, D)) * 1.5 / np.sqrt(D) / s[None, :, None]),
        "a_skip": bf((1.0 + 0.25 * np.random.standard_normal((M, D))) * (t / s)),
        "g_silu": bf((1.0 + 0.25 * np.random.standard_normal((M, D))) * t),
        "w_head": bf(np.random.standard_normal((M, D, V)) * SPREAD / np.sqrt(D) / t[None, :, None]),
        "temp": bf(np.random.uniform(0.5, 1.5, N)),
    }


def stable_log_softmax(z):
    z_max = np.max(z, axis=-1, keepdims=True)
    lse = z_max + np.log(np.sum(np.exp(z - z_max), axis=-1, keepdims=True))
    return z - lse


def stable_softplus(x):
    return np.maximum(x, 0.0) + np.log(1.0 + np.exp(-np.abs(x)))


def sigmoid(x):
    return 1.0 / (1.0 + np.exp(-x))


def core(h, w_res, a_skip, g_silu, w_head, temp):
    h, a_skip, g_silu, temp = f64(h), f64(a_skip), f64(g_silu), f64(temp)

    u = mxq(h, 1, "e4m3") @ mxq(f64(w_res), 1, "e4m3")

    r = a_skip[:, None, :] * h[None, :, :] + g_silu[:, None, :] * u * sigmoid(u)

    z = (mxq(r, 2, "e4m3") @ mxq(f64(w_head), 1, "e4m3")) / temp[None, :, None]

    logp = stable_log_softmax(z)

    ent = -np.sum(np.exp(logp) * logp, axis=-1)

    thr = np.minimum(np.log(EPS), np.log(DELTA) - ent)

    return -stable_softplus(-(logp - thr[:, :, None]) / 2.0)


def e4m3fn_bytes(y):
    return np.clip(np.asarray(y, np.float64), -448.0, 448.0).astype(np.float32).astype(ml_dtypes.float8_e4m3fn).view(np.uint8)


def e4m3fn_values(b):
    return np.asarray(b, np.uint8).view(ml_dtypes.float8_e4m3fn).astype(np.float64)


def setup_inputs():
    d = draw0()
    x0 = np.asarray(d['w_res']).astype(np.float64)
    s = (np.max(np.abs(x0), axis=(0, 2), keepdims=True) / 448.0).astype(np.float32)
    out = {}
    for k, v in d.items():
        if k == 'w_res':
            out['w_res_bytes'] = e4m3fn_bytes(x0 / s.astype(np.float64))
            out['w_res_scale'] = s
        else:
            out[k] = v
    return out


def reference(h, w_res_bytes, w_res_scale, a_skip, g_silu, w_head, temp):
    return core(h, e4m3fn_values(w_res_bytes) * w_res_scale.astype(np.float64), a_skip, g_silu, w_head, temp)

@@ -1,0 +1,454 @@
+import math
+from contextlib import ExitStack
+
+import concourse.mybir as mybir
+from concourse.masks import make_identity
+
+HEADS, TOKENS, D, V = 2, 4096, 512, 512
+EPS, DELTA = 0.001, 0.3
+FLOPS = 2 * HEADS * 2 * TOKENS * D * D
+
+P = 128
+PACK = 4
+GROUP_TILES = 4
+GROUP = GROUP_TILES * P
+GROUPS = TOKENS // GROUP
+TILES_PER_HEAD = TOKENS // P
+UNITS = GROUPS * HEADS
+TILES = UNITS * GROUP_TILES
+CHUNKS = ((0, 32), (32, 64))
+PE_SLOTS = 3
+
+INTER_V = 256
+INTER_S = 512
+
+F32 = mybir.dt.float32
+BF16 = mybir.dt.bfloat16
+U32 = mybir.dt.uint32
+U8 = mybir.dt.uint8
+FP8 = mybir.dt.float8_e4m3fn
+FP8X4 = mybir.dt.float8_e4m3fn_x4
+ALU = mybir.AluOpType
+ACT = mybir.ActivationFunctionType
+
+
+def tile_medusatypicalacceptanceheads_t_kernel(
+    tc, h, w_res_bytes, w_res_scale, a_skip, g_silu, w_head, temp, out
+):
+    nc = tc.nc
+    with ExitStack() as ctx:
+        const = ctx.enter_context(tc.tile_pool(name="const", bufs=1))
+        work = ctx.enter_context(tc.tile_pool(name="work", bufs=36))
+        hq_pool = ctx.enter_context(tc.tile_pool(name="hq_pool", bufs=3))
+        rq_pool = ctx.enter_context(tc.tile_pool(name="rq_pool", bufs=UNITS))
+        side = ctx.enter_context(tc.tile_pool(name="side", bufs=2))
+        e_pool = ctx.enter_context(tc.tile_pool(name="e_pool", bufs=4))
+        stat = ctx.enter_context(tc.tile_pool(name="stat", bufs=4))
+        psum_x = ctx.enter_context(tc.psum_pool(name="psum_x", bufs=2))
+        psum_m = ctx.enter_context(tc.psum_pool(name="psum_m", bufs=6))
+        ctx.enter_context(tc.manual_schedule())
+
+        def work_tile(shape, dtype, name):
+            return work.tile(shape, dtype, name=name, tag="work", align_bytes=64)
+
+        h_view = h.rearrange("(p c) d -> p c d", c=TILES_PER_HEAD)
+        w_bytes, h_raw, wh_raw = [], {}, []
+
+        def load_w_bytes(m):
+            t = const.tile([P, PACK, D], U8, name="w_bytes%d" % m)
+            nc.sync.dma_start(out=t[:], in_=w_res_bytes[m].rearrange("(p t) n -> p t n", t=PACK))
+            w_bytes.append(t)
+
+        def load_h(g, pieces):
+            t = work_tile([P, GROUP_TILES, D], BF16, "h_raw")
+            step = GROUP_TILES // pieces
+            for k in range(0, GROUP_TILES, step):
+                c0 = g * GROUP_TILES + k
+                nc.sync.dma_start(out=t[:, k : k + step, :], in_=h_view[:, c0 : c0 + step, :])
+            h_raw[g] = t
+
+        def load_w_head(m):
+            t = work_tile([P, PACK, V], BF16, "wh_raw")
+            nc.sync.dma_start(out=t[:], in_=w_head[m].rearrange("(p j) v -> p j v", j=PACK))
+            wh_raw.append(t)
+
+        w_scale = const.tile([P, PACK], F32)
+        nc.scalar.dma_start(out=w_scale[:], in_=w_res_scale.rearrange("o (p t) u -> p (o t u)", t=PACK))
+        load_w_bytes(0)
+        load_h(0, 2)
+        a_raw = const.tile([P, HEADS, PACK], BF16)
+        nc.scalar.dma_start(out=a_raw[:], in_=a_skip.rearrange("m (p t) -> p m t", t=PACK))
+        g_raw = const.tile([P, HEADS, PACK], BF16)
+        nc.scalar.dma_start(out=g_raw[:], in_=g_silu.rearrange("m (p t) -> p m t", t=PACK))
+        temp_raw = const.tile([P, TILES_PER_HEAD], BF16)
+        nc.scalar.dma_start(out=temp_raw[:], in_=temp.rearrange("(p c) -> p c", c=TILES_PER_HEAD))
+        load_w_bytes(1)
+        load_h(1, 1)
+        load_h(2, 1)
+        load_w_head(0)
+        load_h(3, 1)
+        load_w_head(1)
+        for g in range(4, GROUPS):
+            load_h(g, 1)
+
+        zero = const.tile([P, 1], F32)
+        nc.vector.memset(zero[:], 0.0)
+        warm = const.tile([P, 1], F32)
+        nc.scalar.activation(out=warm[:], in_=zero[:], func=ACT.Silu)
+        half = const.tile([P, GROUP_TILES], F32)
+        nc.vector.memset(half[:], 0.5)
+        ident = const.tile([P, P], F32)
+        make_identity(nc, ident[:])
+        ident_bf = const.tile([P, P], BF16)
+        nc.vector.tensor_copy(out=ident_bf[:], in_=ident[:])
+
+        wq, wq_s, whq, whq_s = [], [], [], []
+        w_wide, w_grp = {}, {}
+
+        def widen(m, slots, on_scalar):
+            if m not in w_wide:
+                w_wide[m] = work_tile([P, PACK, D], BF16, "w_wide")
+            for t in slots:
+                src = w_bytes[m][:, t, :].bitcast(FP8)
+                if on_scalar:
+                    nc.scalar.activation(out=w_wide[m][:, t, :], in_=src, func=ACT.Copy, scale=w_scale[:, t : t + 1])
+                else:
+                    nc.vector.tensor_scalar(
+                        out=w_wide[m][:, t, :], in0=src, scalar1=w_scale[:, t : t + 1], scalar2=None, op0=ALU.mult
+                    )
+
+        def group_w(m, lo, hi, copy):
+            if m not in w_grp:
+                w_grp[m] = work_tile([P, PACK, P, PACK], BF16, "w_grp")
+            copy(
+                out=w_grp[m][:, lo:hi, :, :],
+                in_=w_wide[m][:].rearrange("p j (m t) -> p t m j", t=PACK)[:, lo:hi, :, :],
+            )
+
+        def quantize_w(m):
+            q = const.tile([P, D], U32, name="w_codes%d" % m, align_bytes=64)
+            s = const.tile([P, D], U8, name="w_scales%d" % m, align_bytes=64)
+            nc.vector.quantize_mx(
+                out=q[:].bitcast(FP8X4), scales=s[:], in_=w_grp[m][:].rearrange("p t m j -> p (t m j)")
+            )
+            wq.append(q)
+            wq_s.append(s)
+
+        wh_grp = {}
+
+        def group_w_head(m):
+            t = work_tile([P, V, PACK], BF16, "wh_grp")
+            nc.gpsimd.tensor_scalar(
+                out=t[:], in0=wh_raw[m][:].rearrange("p j v -> p v j"), scalar1=1.0, scalar2=0.0,
+                op0=ALU.mult, op1=ALU.add,
+            )
+            wh_grp[m] = t
+
+        def quantize_w_head(m):
+            q = const.tile([P, V], U32, name="wh_codes%d" % m, align_bytes=64)
+            s = const.tile([P, V], U8, name="wh_scales%d" % m, align_bytes=64)
+            nc.vector.quantize_mx(
+                out=q[:].bitcast(FP8X4), scales=s[:], in_=wh_grp[m][:].rearrange("p v j -> p (v j)")
+            )
+            whq.append(q)
+            whq_s.append(s)
+
+        h_t, h_q, h_s, x_banks = {}, {}, {}, {}
+
+        def transpose_h(g, b):
+            xt = psum_x.tile([P, 2, 2, P], F32, name="xt")
+            for c in range(2):
+                words = h_raw[g][:, 2 * b + c, :].bitcast(F32)
+                for u in range(2):
+                    nc.tensor.transpose(xt[:, c, u, :], words[:, u : D // 2 : 2], ident[:])
+            x_banks[g, b] = xt
+
+        def empty_h(g, b, copy):
+            if g not in h_t:
+                h_t[g] = work_tile([P, GROUP, PACK], BF16, "h_t")
+            words = h_t[g][:].rearrange("p n j -> p (n j)").bitcast(F32)
+            copy(
+                out=words[:, GROUP * b : GROUP * (b + 1)].rearrange("p (c r u) -> p c r u", c=2, u=2),
+                in_=x_banks[g, b][:].rearrange("p c u r -> p c r u"),
+            )
+
+        def quantize_h(g):
+            q = hq_pool.tile([P, GROUP], U32, name="h_codes", align_bytes=64)
+            s = hq_pool.tile([P, GROUP], U8, name="h_scales", align_bytes=64)
+            nc.vector.quantize_mx(
+                out=q[:].bitcast(FP8X4), scales=s[:], in_=h_t[g][:].rearrange("p n j -> p (n j)")
+            )
+            h_q[g], h_s[g] = q, s
+
+        skip3 = {}
+
+        def skip_last(i):
+            g, m = divmod(i, HEADS)
+            t = side.tile([P, GROUP], F32, name="skip")
+            col = m * PACK + PACK - 1
+            nc.gpsimd.tensor_scalar(
+                out=t[:], in0=h_t[g][:, :, PACK - 1], scalar1=a32[:, col : col + 1], scalar2=0.0,
+                op0=ALU.mult, op1=ALU.add,
+            )
+            skip3[i] = t
+
+        widen(0, (0, 1), True)
+        widen(0, (2, 3), False)
+        transpose_h(0, 0)
+        transpose_h(0, 1)
+        group_w(0, 0, 2, nc.vector.tensor_copy)
+        group_w(0, 2, 4, nc.scalar.copy)
+        empty_h(0, 0, nc.vector.tensor_copy)
+        empty_h(0, 1, nc.scalar.copy)
+        a32 = const.tile([P, HEADS * PACK], F32)
+        nc.vector.tensor_copy(out=a32[:], in_=a_raw[:].rearrange("p m t -> p (m t)"))
+        g32 = const.tile([P, HEADS * PACK], F32)
+        nc.vector.tensor_copy(out=g32[:], in_=g_raw[:].rearrange("p m t -> p (m t)"))
+        quantize_w(0)
+        quantize_h(0)
+        skip_last(0)
+        diag = const.tile([P, HEADS, PE_SLOTS, P], BF16)
+
+        def make_diag(m):
+            for t in range(PE_SLOTS):
+                col = m * PACK + t
+                nc.vector.tensor_scalar(
+                    out=diag[:, m, t, :], in0=ident_bf[:], scalar1=a32[:, col : col + 1], scalar2=None, op0=ALU.mult
+                )
+
+        make_diag(0)
+        widen(1, (0, 1), True)
+        widen(1, (2, 3), False)
+        make_diag(1)
+        group_w(1, 0, 4, nc.vector.tensor_copy)
+        two_temp = const.tile([P, TILES_PER_HEAD], F32)
+        nc.vector.tensor_scalar(out=two_temp[:], in0=temp_raw[:], scalar1=2.0, scalar2=None, op0=ALU.mult)
+        quantize_w(1)
+        inv2t = const.tile([P, TILES_PER_HEAD], F32)
+        nc.vector.reciprocal(out=inv2t[:], in_=two_temp[:])
+
+        r_cols, r_grp, r_q, r_s = {}, {}, {}, {}
+        s_pair = {}
+
+        def stage1(i, t):
+            g, m = divmod(i, HEADS)
+            col = m * PACK + t
+            u = psum_m.tile([P, GROUP], F32, name="bank")
+            nc.tensor.matmul_mx(
+                out=u[:],
+                lhsT=wq[m][:, t * P : (t + 1) * P].bitcast(FP8X4),
+                lhsT_scale=wq_s[m][:, t * P : (t + 1) * P],
+                rhs=h_q[g][:].bitcast(FP8X4),
+                rhs_scale=h_s[g][:],
+                start=True,
+                stop=True,
+            )
+            if t < PE_SLOTS:
+                skip = psum_m.tile([P, GROUP], F32, name="bank")
+                nc.tensor.matmul(skip[:], diag[:, m, t, :], h_t[g][:, :, t], start=True, stop=True)
+            else:
+                skip = skip3[i]
+            if t % 2 == 0:
+                s_pair[i] = work_tile([P, 2, GROUP], F32, "s_pair")
+            s = s_pair[i][:, t % 2, :]
+            nc.scalar.activation(out=s, in_=u[:], func=ACT.Silu)
+            if t == 0:
+                r_cols[i] = work_tile([P, PACK, GROUP], BF16, "r_cols")
+            nc.vector.scalar_tensor_tensor(
+                out=r_cols[i][:, t, :], in0=s, scalar=g32[:, col : col + 1], in1=skip[:], op0=ALU.mult, op1=ALU.add
+            )
+
+        def inter(i, lo, hi, eng):
+            if hi <= lo:
+                return
+            if i not in r_grp:
+                r_grp[i] = work_tile([P, GROUP, PACK], BF16, "r_grp")
+            dst = r_grp[i][:, lo:hi, :]
+            src = r_cols[i][:].rearrange("p t n -> p n t")[:, lo:hi, :]
+            if eng == 0:
+                nc.vector.tensor_copy(out=dst, in_=src)
+            elif eng == 1:
+                nc.scalar.copy(out=dst, in_=src)
+            else:
+                nc.gpsimd.tensor_scalar(
+                    out=dst, in0=src, scalar1=1.0, scalar2=0.0, op0=ALU.mult, op1=ALU.add
+                )
+
+        def quantize_r(i):
+            q = rq_pool.tile([P, GROUP], U32, name="r_codes", align_bytes=64)
+            s = rq_pool.tile([P, GROUP], U8, name="r_scales", align_bytes=64)
+            nc.vector.quantize_mx(
+                out=q[:].bitcast(FP8X4), scales=s[:], in_=r_grp[i][:].rearrange("p n j -> p (n j)")
+            )
+            r_q[i], r_s[i] = q, s
+
+        m2 = const.tile([P, TILES], F32)
+        nm2 = const.tile([P, TILES], F32)
+        sums = const.tile([P, TILES], F32)
+        ents = const.tile([P, TILES], F32)
+        dd = const.tile([P, TILES], F32)
+        y_pair, w_pair, e_tile = {}, {}, {}
+
+        def logits(j):
+            i, c = divmod(j, GROUP_TILES)
+            g, m = divmod(i, HEADS)
+            z = psum_m.tile([P, V], F32, name="bank")
+            nc.tensor.matmul_mx(
+                out=z[:],
+                lhsT=r_q[i][:, c * P : (c + 1) * P].bitcast(FP8X4),
+                lhsT_scale=r_s[i][:, c * P : (c + 1) * P],
+                rhs=whq[m][:].bitcast(FP8X4),
+                rhs_scale=whq_s[m][:],
+                start=True,
+                stop=True,
+            )
+            if j % 2 == 0:
+                y_pair[j // 2] = work_tile([P, 2, V], F32, "y_pair")
+            col = g * GROUP_TILES + c
+            nc.vector.tensor_scalar(
+                out=y_pair[j // 2][:, j % 2, :], in0=z[:], scalar1=inv2t[:, col : col + 1], scalar2=None,
+                op0=ALU.mult, op1=ALU.max, accum_out=m2[:, j : j + 1],
+            )
+            if j % 2 == 1:
+                nc.gpsimd.tensor_scalar(
+                    out=nm2[:, j - 1 : j + 1], in0=m2[:, j - 1 : j + 1], scalar1=-1.0, scalar2=0.0,
+                    op0=ALU.mult, op1=ALU.add,
+                )
+
+        def expo(j):
+            if j % 2 == 0:
+                w_pair[j // 2] = work_tile([P, 2, V], F32, "w_pair")
+            nc.scalar.activation(
+                out=w_pair[j // 2][:, j % 2, :], in_=y_pair[j // 2][:, j % 2, :], func=ACT.Exp,
+                bias=nm2[:, j : j + 1],
+            )
+
+        def squares(j):
+            e_tile[j] = e_pool.tile([P, V], F32, name="e")
+            nc.scalar.activation(
+                out=e_tile[j][:], in_=w_pair[j // 2][:, j % 2, :], func=ACT.Square, accum_out=sums[:, j : j + 1]
+            )
+
+        def weighted(j):
+            e = e_tile[j]
+            nc.vector.scalar_tensor_tensor(
+                out=e[:], in0=y_pair[j // 2][:, j % 2, :], scalar=nm2[:, j : j + 1], in1=e[:],
+                op0=ALU.add, op1=ALU.mult, accum_out=ents[:, j : j + 1],
+            )
+
+        st = {}
+
+        def unit(i):
+            return slice(i * GROUP_TILES, (i + 1) * GROUP_TILES)
+
+        def thr_a(i):
+            st[i, "r"] = stat.tile([P, GROUP_TILES], F32, name="rec")
+            nc.vector.reciprocal(out=st[i, "r"][:], in_=sums[:, unit(i)])
+            sm = stat.tile([P, GROUP_TILES], F32, name="sm")
+            nc.gpsimd.tensor_scalar(
+                out=sm[:], in0=sums[:, unit(i)], scalar1=EPS, scalar2=0.0, op0=ALU.mult, op1=ALU.add
+            )
+            st[i, "root"] = stat.tile([P, GROUP_TILES], F32, name="root")
+            nc.gpsimd.tensor_tensor(out=st[i, "root"][:], in0=sm[:], in1=half[:], op=ALU.pow)
+
+        def thr_b(i):
+            st[i, "q"] = stat.tile([P, GROUP_TILES], F32, name="q")
+            nc.vector.tensor_tensor(out=st[i, "q"][:], in0=ents[:, unit(i)], in1=st[i, "r"][:], op=ALU.mult)
+
+        def thr_c(i):
+            st[i, "x"] = stat.tile([P, GROUP_TILES], F32, name="xq")
+            nc.scalar.activation(out=st[i, "x"][:], in_=st[i, "q"][:], func=ACT.Exp)
+
+        def thr_d(i):
+            nc.vector.scalar_tensor_tensor(
+                out=dd[:, unit(i)], in0=st[i, "x"][:], scalar=math.sqrt(DELTA), in1=st[i, "root"][:],
+                op0=ALU.mult, op1=ALU.min,
+            )
+
+        def lnp(j):
+            w = w_pair[j // 2][:, j % 2, :]
+            nc.scalar.activation(out=w, in_=w, func=ACT.Ln, bias=dd[:, j : j + 1])
+
+        def final(j):
+            y = y_pair[j // 2][:, j % 2, :]
+            nc.vector.scalar_tensor_tensor(
+                out=y, in0=y, scalar=nm2[:, j : j + 1], in1=w_pair[j // 2][:, j % 2, :],
+                op0=ALU.add, op1=ALU.subtract,
+            )
+            if j % 2 == 1:
+                i, c = divmod(j - 1, GROUP_TILES)
+                g, m = divmod(i, HEADS)
+                c0 = g * GROUP_TILES + c
+                nc.sync.dma_start(
+                    out=out[m].rearrange("(p c) v -> p c v", c=TILES_PER_HEAD)[:, c0 : c0 + 2, :],
+                    in_=y_pair[j // 2][:],
+                )
+
+        for i in range(UNITS):
+            g, m = divmod(i, HEADS)
+            nxt = g + 1 < GROUPS
+            stage1(i, 0)
+            if i > 0:
+                inter(i - 1, 0, INTER_V, 0)
+                inter(i - 1, INTER_S, GROUP, 2)
+            if m == 1 and nxt:
+                empty_h(g + 1, 1, nc.scalar.copy)
+            stage1(i, 1)
+            if m == 0:
+                skip_last(i + 1)
+            if i in (2, 4):
+                group_w_head(i // 2 - 1)
+            stage1(i, 2)
+            if i > 0:
+                inter(i - 1, INTER_V, INTER_S, 1)
+            if m == 0 and nxt:
+                transpose_h(g + 1, 0)
+            if m == 1 and nxt:
+                quantize_h(g + 1)
+            if i in (5, 7):
+                quantize_w_head((i - 5) // 2)
+            stage1(i, 3)
+            if m == 0 and nxt:
+                transpose_h(g + 1, 1)
+                empty_h(g + 1, 0, nc.scalar.copy)
+            if m == 1 and nxt:
+                skip_last(i + 1)
+            if i > 0:
+                quantize_r(i - 1)
+
+        last = UNITS - 1
+        logits(0)
+        inter(last, 0, INTER_V, 0)
+        inter(last, INTER_S, GROUP, 2)
+        inter(last, INTER_V, INTER_S, 1)
+        logits(1)
+        logits(2)
+        logits(3)
+        quantize_r(last)
+        done = 4
+
+        for start, end in CHUNKS:
+            for j in range(start, end + 8):
+                while done < min(j + 4, end + 4, TILES):
+                    logits(done)
+                    done += 1
+                if j < end:
+                    expo(j)
+                if start <= j - 1 < end:
+                    squares(j - 1)
+                k = j - 4
+                if start <= k < end and k % GROUP_TILES == 3:
+                    thr_a(k // GROUP_TILES)
+                if start <= j - 3 < end:
+                    weighted(j - 3)
+                if start <= k < end and k % GROUP_TILES == 3:
+                    thr_b(k // GROUP_TILES)
+                k = j - 5
+                if start <= k < end and k % GROUP_TILES == 3:
+                    thr_c(k // GROUP_TILES)
+                k = j - 6
+                if start <= k < end and k % GROUP_TILES == 3:
+                    thr_d(k // GROUP_TILES)
+            for j in range(start, end):
+                lnp(j)
+                final(j)

@@ -16,10 +16,15 @@ GROUPS = TOKENS // GROUP
 TILES_PER_HEAD = TOKENS // P
 UNITS = GROUPS * HEADS
 TILES = UNITS * GROUP_TILES
-CHUNKS = ((0, 32), (32, 64))
+CHUNKS = ((0, 24), (24, 64))
+LOOK = 6
+EXTRA = 2
+LAG = 4
+AHEAD = 2
+PRE = {10: 1, 11: 1, 12: 1, 13: 1, 14: 1, 15: 1}
 PE_SLOTS = 3
 
-INTER_V = 256
+INTER_V = 176
 INTER_S = 512
 
 F32 = mybir.dt.float32
@@ -38,14 +43,15 @@ def tile_medusatypicalacceptanceheads_t_kernel(
     nc = tc.nc
     with ExitStack() as ctx:
         const = ctx.enter_context(tc.tile_pool(name="const", bufs=1))
-        work = ctx.enter_context(tc.tile_pool(name="work", bufs=36))
-        hq_pool = ctx.enter_context(tc.tile_pool(name="hq_pool", bufs=3))
+        work = ctx.enter_context(tc.tile_pool(name="work", bufs=40))
+        hq_pool = ctx.enter_context(tc.tile_pool(name="hq_pool", bufs=2))
         rq_pool = ctx.enter_context(tc.tile_pool(name="rq_pool", bufs=UNITS))
         side = ctx.enter_context(tc.tile_pool(name="side", bufs=2))
-        e_pool = ctx.enter_context(tc.tile_pool(name="e_pool", bufs=4))
+        e_pool = ctx.enter_context(tc.tile_pool(name="e_pool", bufs=5))
         stat = ctx.enter_context(tc.tile_pool(name="stat", bufs=4))
         psum_x = ctx.enter_context(tc.psum_pool(name="psum_x", bufs=2))
-        psum_m = ctx.enter_context(tc.psum_pool(name="psum_m", bufs=6))
+        psum_u = ctx.enter_context(tc.psum_pool(name="psum_u", bufs=3))
+        psum_s = ctx.enter_context(tc.psum_pool(name="psum_s", bufs=3))
         ctx.enter_context(tc.manual_schedule())
 
         def work_tile(shape, dtype, name):
@@ -95,8 +101,6 @@ def tile_medusatypicalacceptanceheads_t_kernel(
         nc.vector.memset(zero[:], 0.0)
         warm = const.tile([P, 1], F32)
         nc.scalar.activation(out=warm[:], in_=zero[:], func=ACT.Silu)
-        half = const.tile([P, GROUP_TILES], F32)
-        nc.vector.memset(half[:], 0.5)
         ident = const.tile([P, P], F32)
         make_identity(nc, ident[:])
         ident_bf = const.tile([P, P], BF16)
@@ -138,9 +142,8 @@ def tile_medusatypicalacceptanceheads_t_kernel(
 
         def group_w_head(m):
             t = work_tile([P, V, PACK], BF16, "wh_grp")
-            nc.gpsimd.tensor_scalar(
-                out=t[:], in0=wh_raw[m][:].rearrange("p j v -> p v j"), scalar1=1.0, scalar2=0.0,
-                op0=ALU.mult, op1=ALU.add,
+            nc.vector.tensor_copy(
+                out=t[:].rearrange("p (c i) j -> p c j i", i=4), in_=wh_raw[m][:].rearrange("p j (c i) -> p c j i", i=4)
             )
             wh_grp[m] = t
 
@@ -186,9 +189,8 @@ def tile_medusatypicalacceptanceheads_t_kernel(
             g, m = divmod(i, HEADS)
             t = side.tile([P, GROUP], F32, name="skip")
             col = m * PACK + PACK - 1
-            nc.gpsimd.tensor_scalar(
-                out=t[:], in0=h_t[g][:, :, PACK - 1], scalar1=a32[:, col : col + 1], scalar2=0.0,
-                op0=ALU.mult, op1=ALU.add,
+            nc.vector.tensor_scalar(
+                out=t[:], in0=h_t[g][:, :, PACK - 1], scalar1=a32[:, col : col + 1], scalar2=None, op0=ALU.mult
             )
             skip3[i] = t
 
@@ -230,10 +232,14 @@ def tile_medusatypicalacceptanceheads_t_kernel(
         r_cols, r_grp, r_q, r_s = {}, {}, {}, {}
         s_pair = {}
 
-        def stage1(i, t):
+        u_bank = {}
+
+        def project(k):
+            if k >= UNITS * PACK:
+                return
+            i, t = divmod(k, PACK)
             g, m = divmod(i, HEADS)
-            col = m * PACK + t
-            u = psum_m.tile([P, GROUP], F32, name="bank")
+            u = psum_u.tile([P, GROUP], F32, name="u_bank")
             nc.tensor.matmul_mx(
                 out=u[:],
                 lhsT=wq[m][:, t * P : (t + 1) * P].bitcast(FP8X4),
@@ -243,15 +249,22 @@ def tile_medusatypicalacceptanceheads_t_kernel(
                 start=True,
                 stop=True,
             )
+            u_bank[k] = u
+
+        def stage1(i, t):
+            g, m = divmod(i, HEADS)
+            k = i * PACK + t
+            col = m * PACK + t
+            project(k + AHEAD)
             if t < PE_SLOTS:
-                skip = psum_m.tile([P, GROUP], F32, name="bank")
+                skip = psum_s.tile([P, GROUP], F32, name="s_bank")
                 nc.tensor.matmul(skip[:], diag[:, m, t, :], h_t[g][:, :, t], start=True, stop=True)
             else:
                 skip = skip3[i]
             if t % 2 == 0:
                 s_pair[i] = work_tile([P, 2, GROUP], F32, "s_pair")
             s = s_pair[i][:, t % 2, :]
-            nc.scalar.activation(out=s, in_=u[:], func=ACT.Silu)
+            nc.scalar.activation(out=s, in_=u_bank[k][:], func=ACT.Silu)
             if t == 0:
                 r_cols[i] = work_tile([P, PACK, GROUP], BF16, "r_cols")
             nc.vector.scalar_tensor_tensor(
@@ -263,16 +276,12 @@ def tile_medusatypicalacceptanceheads_t_kernel(
                 return
             if i not in r_grp:
                 r_grp[i] = work_tile([P, GROUP, PACK], BF16, "r_grp")
-            dst = r_grp[i][:, lo:hi, :]
-            src = r_cols[i][:].rearrange("p t n -> p n t")[:, lo:hi, :]
+            dst = r_grp[i][:, lo:hi, :].rearrange("p (c i) t -> p c t i", i=4)
+            src = r_cols[i][:, :, lo:hi].rearrange("p t (c i) -> p c t i", i=4)
             if eng == 0:
                 nc.vector.tensor_copy(out=dst, in_=src)
-            elif eng == 1:
-                nc.scalar.copy(out=dst, in_=src)
             else:
-                nc.gpsimd.tensor_scalar(
-                    out=dst, in0=src, scalar1=1.0, scalar2=0.0, op0=ALU.mult, op1=ALU.add
-                )
+                nc.scalar.copy(out=dst, in_=src)
 
         def quantize_r(i):
             q = rq_pool.tile([P, GROUP], U32, name="r_codes", align_bytes=64)
@@ -292,7 +301,10 @@ def tile_medusatypicalacceptanceheads_t_kernel(
         def logits(j):
             i, c = divmod(j, GROUP_TILES)
             g, m = divmod(i, HEADS)
-            z = psum_m.tile([P, V], F32, name="bank")
+            if j % 2 == 0:
+                z = psum_u.tile([P, V], F32, name="u_bank")
+            else:
+                z = psum_s.tile([P, V], F32, name="s_bank")
             nc.tensor.matmul_mx(
                 out=z[:],
                 lhsT=r_q[i][:, c * P : (c + 1) * P].bitcast(FP8X4),
@@ -309,13 +321,10 @@ def tile_medusatypicalacceptanceheads_t_kernel(
                 out=y_pair[j // 2][:, j % 2, :], in0=z[:], scalar1=inv2t[:, col : col + 1], scalar2=None,
                 op0=ALU.mult, op1=ALU.max, accum_out=m2[:, j : j + 1],
             )
-            if j % 2 == 1:
-                nc.gpsimd.tensor_scalar(
-                    out=nm2[:, j - 1 : j + 1], in0=m2[:, j - 1 : j + 1], scalar1=-1.0, scalar2=0.0,
-                    op0=ALU.mult, op1=ALU.add,
-                )
 
         def expo(j):
+            if j % GROUP_TILES == 0:
+                nc.scalar.mul(nm2[:, j : j + GROUP_TILES], m2[:, j : j + GROUP_TILES], -1.0)
             if j % 2 == 0:
                 w_pair[j // 2] = work_tile([P, 2, V], F32, "w_pair")
             nc.scalar.activation(
@@ -332,8 +341,8 @@ def tile_medusatypicalacceptanceheads_t_kernel(
         def weighted(j):
             e = e_tile[j]
             nc.vector.scalar_tensor_tensor(
-                out=e[:], in0=y_pair[j // 2][:, j % 2, :], scalar=nm2[:, j : j + 1], in1=e[:],
-                op0=ALU.add, op1=ALU.mult, accum_out=ents[:, j : j + 1],
+                out=e[:], in0=y_pair[j // 2][:, j % 2, :], scalar=m2[:, j : j + 1], in1=e[:],
+                op0=ALU.subtract, op1=ALU.mult, accum_out=ents[:, j : j + 1],
             )
 
         st = {}
@@ -341,27 +350,24 @@ def tile_medusatypicalacceptanceheads_t_kernel(
         def unit(i):
             return slice(i * GROUP_TILES, (i + 1) * GROUP_TILES)
 
+        arm = const.tile([P, TILES], F32)
+        root = const.tile([P, TILES], F32)
+
         def thr_a(i):
             st[i, "r"] = stat.tile([P, GROUP_TILES], F32, name="rec")
             nc.vector.reciprocal(out=st[i, "r"][:], in_=sums[:, unit(i)])
-            sm = stat.tile([P, GROUP_TILES], F32, name="sm")
-            nc.gpsimd.tensor_scalar(
-                out=sm[:], in0=sums[:, unit(i)], scalar1=EPS, scalar2=0.0, op0=ALU.mult, op1=ALU.add
-            )
-            st[i, "root"] = stat.tile([P, GROUP_TILES], F32, name="root")
-            nc.gpsimd.tensor_tensor(out=st[i, "root"][:], in0=sm[:], in1=half[:], op=ALU.pow)
 
         def thr_b(i):
             st[i, "q"] = stat.tile([P, GROUP_TILES], F32, name="q")
             nc.vector.tensor_tensor(out=st[i, "q"][:], in0=ents[:, unit(i)], in1=st[i, "r"][:], op=ALU.mult)
 
         def thr_c(i):
-            st[i, "x"] = stat.tile([P, GROUP_TILES], F32, name="xq")
-            nc.scalar.activation(out=st[i, "x"][:], in_=st[i, "q"][:], func=ACT.Exp)
+            nc.scalar.activation(out=arm[:, unit(i)], in_=st[i, "q"][:], func=ACT.Exp)
 
-        def thr_d(i):
+        def thr_d(lo, hi):
+            nc.scalar.activation(out=root[:, lo:hi], in_=sums[:, lo:hi], func=ACT.Sqrt, scale=EPS)
             nc.vector.scalar_tensor_tensor(
-                out=dd[:, unit(i)], in0=st[i, "x"][:], scalar=math.sqrt(DELTA), in1=st[i, "root"][:],
+                out=dd[:, lo:hi], in0=arm[:, lo:hi], scalar=math.sqrt(DELTA), in1=root[:, lo:hi],
                 op0=ALU.mult, op1=ALU.min,
             )
 
@@ -372,8 +378,8 @@ def tile_medusatypicalacceptanceheads_t_kernel(
         def final(j):
             y = y_pair[j // 2][:, j % 2, :]
             nc.vector.scalar_tensor_tensor(
-                out=y, in0=y, scalar=nm2[:, j : j + 1], in1=w_pair[j // 2][:, j % 2, :],
-                op0=ALU.add, op1=ALU.subtract,
+                out=y, in0=y, scalar=m2[:, j : j + 1], in1=w_pair[j // 2][:, j % 2, :],
+                op0=ALU.subtract, op1=ALU.subtract,
             )
             if j % 2 == 1:
                 i, c = divmod(j - 1, GROUP_TILES)
@@ -384,71 +390,76 @@ def tile_medusatypicalacceptanceheads_t_kernel(
                     in_=y_pair[j // 2][:],
                 )
 
+        done = 0
+        for k in range(AHEAD):
+            project(k)
         for i in range(UNITS):
             g, m = divmod(i, HEADS)
             nxt = g + 1 < GROUPS
+            if m == 0 and nxt:
+                transpose_h(g + 1, 0)
+            if m == 0 and nxt:
+                transpose_h(g + 1, 1)
             stage1(i, 0)
+            if i > 1:
+                quantize_r(i - 2)
             if i > 0:
                 inter(i - 1, 0, INTER_V, 0)
-                inter(i - 1, INTER_S, GROUP, 2)
-            if m == 1 and nxt:
-                empty_h(g + 1, 1, nc.scalar.copy)
             stage1(i, 1)
-            if m == 0:
-                skip_last(i + 1)
+            if m == 0 and nxt:
+                empty_h(g + 1, 0, nc.scalar.copy)
             if i in (2, 4):
                 group_w_head(i // 2 - 1)
             stage1(i, 2)
+            if m == 0 and nxt:
+                empty_h(g + 1, 1, nc.scalar.copy)
+            if i in (5, 7):
+                quantize_w_head((i - 5) // 2)
+            if PRE.get(i, 0) > 0:
+                logits(done)
+                done += 1
+            stage1(i, 3)
             if i > 0:
                 inter(i - 1, INTER_V, INTER_S, 1)
             if m == 0 and nxt:
-                transpose_h(g + 1, 0)
-            if m == 1 and nxt:
                 quantize_h(g + 1)
-            if i in (5, 7):
-                quantize_w_head((i - 5) // 2)
-            stage1(i, 3)
-            if m == 0 and nxt:
-                transpose_h(g + 1, 1)
-                empty_h(g + 1, 0, nc.scalar.copy)
-            if m == 1 and nxt:
+            if i + 1 < UNITS:
                 skip_last(i + 1)
-            if i > 0:
-                quantize_r(i - 1)
+            if PRE.get(i, 0) > 1:
+                logits(done)
+                done += 1
 
         last = UNITS - 1
-        logits(0)
         inter(last, 0, INTER_V, 0)
-        inter(last, INTER_S, GROUP, 2)
         inter(last, INTER_V, INTER_S, 1)
-        logits(1)
-        logits(2)
-        logits(3)
+        quantize_r(last - 1)
+        logits(done)
+        logits(done + 1)
+        done += 2
         quantize_r(last)
-        done = 4
-
+        j = 0
         for start, end in CHUNKS:
-            for j in range(start, end + 8):
-                while done < min(j + 4, end + 4, TILES):
+            while j < end + LAG + 2:
+                while done < min(j + LOOK + 1 + EXTRA * max(0, min(j - end + 1, 3)) * (end < TILES), TILES):
                     logits(done)
                     done += 1
-                if j < end:
-                    expo(j)
-                if start <= j - 1 < end:
-                    squares(j - 1)
-                k = j - 4
-                if start <= k < end and k % GROUP_TILES == 3:
-                    thr_a(k // GROUP_TILES)
-                if start <= j - 3 < end:
-                    weighted(j - 3)
-                if start <= k < end and k % GROUP_TILES == 3:
-                    thr_b(k // GROUP_TILES)
-                k = j - 5
-                if start <= k < end and k % GROUP_TILES == 3:
+                k = j - LAG - 2
+                if k >= 0 and k % GROUP_TILES == 3:
                     thr_c(k // GROUP_TILES)
-                k = j - 6
-                if start <= k < end and k % GROUP_TILES == 3:
-                    thr_d(k // GROUP_TILES)
-            for j in range(start, end):
-                lnp(j)
-                final(j)
+                if j < TILES:
+                    expo(j)
+                if 0 < j <= TILES:
+                    squares(j - 1)
+                k = j - LAG - 1
+                if k >= 0 and k % GROUP_TILES == 3:
+                    thr_b(k // GROUP_TILES)
+                k = j - LAG
+                if 0 <= k < TILES:
+                    weighted(k)
+                    if k % GROUP_TILES == 3:
+                        thr_a(k // GROUP_TILES)
+                j += 1
+            thr_d(start, end)
+            for f in range(start, end):
+                lnp(f)
+                final(f)

@@ -24,8 +24,8 @@ AHEAD = 2
 PRE = {10: 1, 11: 1, 12: 1, 13: 1, 14: 1, 15: 1}
 PE_SLOTS = 3
 
-INTER_V = 176
-INTER_S = 512
+INTER_V = 0
+INTER_G = 256
 
 F32 = mybir.dt.float32
 BF16 = mybir.dt.bfloat16
@@ -280,8 +280,12 @@ def tile_medusatypicalacceptanceheads_t_kernel(
             src = r_cols[i][:, :, lo:hi].rearrange("p t (c i) -> p c t i", i=4)
             if eng == 0:
                 nc.vector.tensor_copy(out=dst, in_=src)
-            else:
+            elif eng == 1:
                 nc.scalar.copy(out=dst, in_=src)
+            else:
+                nc.gpsimd.tensor_scalar(
+                    out=dst, in0=src, scalar1=1.0, scalar2=0.0, op0=ALU.mult, op1=ALU.add
+                )
 
         def quantize_r(i):
             q = rq_pool.tile([P, GROUP], U32, name="r_codes", align_bytes=64)
@@ -401,37 +405,40 @@ def tile_medusatypicalacceptanceheads_t_kernel(
             if m == 0 and nxt:
                 transpose_h(g + 1, 1)
             stage1(i, 0)
-            if i > 1:
-                quantize_r(i - 2)
             if i > 0:
-                inter(i - 1, 0, INTER_V, 0)
-            stage1(i, 1)
+                inter(i - 1, INTER_V, INTER_G, 2)
             if m == 0 and nxt:
                 empty_h(g + 1, 0, nc.scalar.copy)
-            if i in (2, 4):
-                group_w_head(i // 2 - 1)
-            stage1(i, 2)
+            stage1(i, 1)
             if m == 0 and nxt:
                 empty_h(g + 1, 1, nc.scalar.copy)
-            if i in (5, 7):
-                quantize_w_head((i - 5) // 2)
-            if PRE.get(i, 0) > 0:
-                logits(done)
-                done += 1
-            stage1(i, 3)
+            stage1(i, 2)
             if i > 0:
-                inter(i - 1, INTER_V, INTER_S, 1)
-            if m == 0 and nxt:
-                quantize_h(g + 1)
+                inter(i - 1, 0, INTER_V, 0)
+            if i > 0:
+                inter(i - 1, INTER_G, GROUP, 1)
             if i + 1 < UNITS:
                 skip_last(i + 1)
+            if m == 0 and nxt:
+                quantize_h(g + 1)
+            if i in (2, 4):
+                group_w_head(i // 2 - 1)
+            if i in (5, 7):
+                quantize_w_head((i - 5) // 2)
             if PRE.get(i, 0) > 1:
+                logits(done)
+                done += 1
+            if i > 1:
+                quantize_r(i - 2)
+            stage1(i, 3)
+            if PRE.get(i, 0) > 0:
                 logits(done)
                 done += 1
 
         last = UNITS - 1
         inter(last, 0, INTER_V, 0)
-        inter(last, INTER_V, INTER_S, 1)
+        inter(last, INTER_V, INTER_G, 2)
+        inter(last, INTER_G, GROUP, 1)
         quantize_r(last - 1)
         logits(done)
         logits(done + 1)

@@ -17,15 +17,17 @@ TILES_PER_HEAD = TOKENS // P
 UNITS = GROUPS * HEADS
 TILES = UNITS * GROUP_TILES
 CHUNKS = ((0, 24), (24, 64))
-LOOK = 6
-EXTRA = 2
+LOOK = 5
+SKIP_M = 1
+X1 = 3
+X2 = 3
 LAG = 4
 AHEAD = 2
-PRE = {10: 1, 11: 1, 12: 1, 13: 1, 14: 1, 15: 1}
+PRE = {12: 1, 13: 1, 14: 1, 15: 1}
 PE_SLOTS = 3
 
 INTER_V = 0
-INTER_G = 256
+INTER_G = 288
 
 F32 = mybir.dt.float32
 BF16 = mybir.dt.bfloat16
@@ -189,9 +191,14 @@ def tile_medusatypicalacceptanceheads_t_kernel(
             g, m = divmod(i, HEADS)
             t = side.tile([P, GROUP], F32, name="skip")
             col = m * PACK + PACK - 1
-            nc.vector.tensor_scalar(
-                out=t[:], in0=h_t[g][:, :, PACK - 1], scalar1=a32[:, col : col + 1], scalar2=None, op0=ALU.mult
-            )
+            if m == SKIP_M:
+                nc.scalar.activation(
+                    out=t[:], in_=h_t[g][:, :, PACK - 1], func=ACT.Copy, scale=a32[:, col : col + 1]
+                )
+            else:
+                nc.vector.tensor_scalar(
+                    out=t[:], in0=h_t[g][:, :, PACK - 1], scalar1=a32[:, col : col + 1], scalar2=None, op0=ALU.mult
+                )
             skip3[i] = t
 
         widen(0, (0, 1), True)
@@ -276,8 +283,12 @@ def tile_medusatypicalacceptanceheads_t_kernel(
                 return
             if i not in r_grp:
                 r_grp[i] = work_tile([P, GROUP, PACK], BF16, "r_grp")
-            dst = r_grp[i][:, lo:hi, :].rearrange("p (c i) t -> p c t i", i=4)
-            src = r_cols[i][:, :, lo:hi].rearrange("p t (c i) -> p c t i", i=4)
+            if eng == 2:
+                dst = r_grp[i][:, lo:hi, :]
+                src = r_cols[i][:, :, lo:hi].rearrange("p t n -> p n t")
+            else:
+                dst = r_grp[i][:, lo:hi, :].rearrange("p (c i) t -> p c t i", i=4)
+                src = r_cols[i][:, :, lo:hi].rearrange("p t (c i) -> p c t i", i=4)
             if eng == 0:
                 nc.vector.tensor_copy(out=dst, in_=src)
             elif eng == 1:
@@ -447,7 +458,7 @@ def tile_medusatypicalacceptanceheads_t_kernel(
         j = 0
         for start, end in CHUNKS:
             while j < end + LAG + 2:
-                while done < min(j + LOOK + 1 + EXTRA * max(0, min(j - end + 1, 3)) * (end < TILES), TILES):
+                while done < min(j + LOOK + 1, end + LAG + 4, TILES):
                     logits(done)
                     done += 1
                 k = j - LAG - 2
@@ -466,7 +477,15 @@ def tile_medusatypicalacceptanceheads_t_kernel(
                     if k % GROUP_TILES == 3:
                         thr_a(k // GROUP_TILES)
                 j += 1
+            if end < TILES:
+                for f in range(X1):
+                    logits(done)
+                    done += 1
             thr_d(start, end)
+            if end < TILES:
+                for f in range(X2):
+                    logits(done)
+                    done += 1
             for f in range(start, end):
                 lnp(f)
                 final(f)

@@ -6,28 +6,25 @@ from concourse.masks import make_identity
 
 HEADS, TOKENS, D, V = 2, 4096, 512, 512
 EPS, DELTA = 0.001, 0.3
-FLOPS = 2 * HEADS * 2 * TOKENS * D * D
+FLOPS = 2 * HEADS * TOKENS * D * (D + V)
 
 P = 128
 PACK = 4
-GROUP_TILES = 4
-GROUP = GROUP_TILES * P
+TOKEN_COLS = TOKENS // P
+GROUP_COLS = 4
+GROUP = GROUP_COLS * P
 GROUPS = TOKENS // GROUP
-TILES_PER_HEAD = TOKENS // P
 UNITS = GROUPS * HEADS
-TILES = UNITS * GROUP_TILES
-CHUNKS = ((0, 24), (24, 64))
-LOOK = 5
-SKIP_M = 1
-X1 = 3
-X2 = 3
-LAG = 4
-AHEAD = 2
-PRE = {12: 1, 13: 1, 14: 1, 15: 1}
-PE_SLOTS = 3
+TILES = UNITS * GROUP_COLS
 
-INTER_V = 0
-INTER_G = 288
+TENSOR_SLOTS = 3
+GPSIMD_COLS = 256
+PROJECT_AHEAD = 2
+SWEEPS = ((0, 24), (24, 64))
+WORK_BUFS = 40
+LOOK, LAG = 5, 4
+EARLY_UNITS, EARLY_LAST = 4, 2
+BRIDGE_BEFORE, BRIDGE_AFTER = 3, 3
 
 F32 = mybir.dt.float32
 BF16 = mybir.dt.bfloat16
@@ -45,13 +42,13 @@ def tile_medusatypicalacceptanceheads_t_kernel(
     nc = tc.nc
     with ExitStack() as ctx:
         const = ctx.enter_context(tc.tile_pool(name="const", bufs=1))
-        work = ctx.enter_context(tc.tile_pool(name="work", bufs=40))
-        hq_pool = ctx.enter_context(tc.tile_pool(name="hq_pool", bufs=2))
-        rq_pool = ctx.enter_context(tc.tile_pool(name="rq_pool", bufs=UNITS))
-        side = ctx.enter_context(tc.tile_pool(name="side", bufs=2))
-        e_pool = ctx.enter_context(tc.tile_pool(name="e_pool", bufs=5))
-        stat = ctx.enter_context(tc.tile_pool(name="stat", bufs=4))
-        psum_x = ctx.enter_context(tc.psum_pool(name="psum_x", bufs=2))
+        work = ctx.enter_context(tc.tile_pool(name="work", bufs=WORK_BUFS))
+        h_mx_pool = ctx.enter_context(tc.tile_pool(name="h_mx_pool", bufs=2))
+        r_mx_pool = ctx.enter_context(tc.tile_pool(name="r_mx_pool", bufs=UNITS))
+        skip_pool = ctx.enter_context(tc.tile_pool(name="skip_pool", bufs=2))
+        square_pool = ctx.enter_context(tc.tile_pool(name="square_pool", bufs=LAG + 1))
+        stat_pool = ctx.enter_context(tc.tile_pool(name="stat_pool", bufs=4))
+        psum_t = ctx.enter_context(tc.psum_pool(name="psum_t", bufs=2))
         psum_u = ctx.enter_context(tc.psum_pool(name="psum_u", bufs=3))
         psum_s = ctx.enter_context(tc.psum_pool(name="psum_s", bufs=3))
         ctx.enter_context(tc.manual_schedule())
@@ -59,26 +56,43 @@ def tile_medusatypicalacceptanceheads_t_kernel(
         def work_tile(shape, dtype, name):
             return work.tile(shape, dtype, name=name, tag="work", align_bytes=64)
 
-        h_view = h.rearrange("(p c) d -> p c d", c=TILES_PER_HEAD)
-        w_bytes, h_raw, wh_raw = [], {}, []
+        def quantize(pool, name, grouped):
+            codes = pool.tile([P, 512], U32, name=name + "_codes", align_bytes=64)
+            scales = pool.tile([P, 512], U8, name=name + "_scales", align_bytes=64)
+            nc.vector.quantize_mx(out=codes[:].bitcast(FP8X4), scales=scales[:], in_=grouped)
+            return codes, scales
+
+        def matmul_mx(bank, stationary, cols, moving):
+            nc.tensor.matmul_mx(
+                out=bank[:],
+                lhsT=stationary[0][:, cols].bitcast(FP8X4),
+                lhsT_scale=stationary[1][:, cols],
+                rhs=moving[0][:].bitcast(FP8X4),
+                rhs_scale=moving[1][:],
+                start=True,
+                stop=True,
+            )
+
+        h_view = h.rearrange("(p c) d -> p c d", c=TOKEN_COLS)
+        w_bytes, h_raw, w_head_raw = [], [], []
 
         def load_w_bytes(m):
-            t = const.tile([P, PACK, D], U8, name="w_bytes%d" % m)
-            nc.sync.dma_start(out=t[:], in_=w_res_bytes[m].rearrange("(p t) n -> p t n", t=PACK))
-            w_bytes.append(t)
+            tile = const.tile([P, PACK, D], U8, name="w_bytes%d" % m)
+            nc.sync.dma_start(out=tile[:], in_=w_res_bytes[m].rearrange("(p t) n -> p t n", t=PACK))
+            w_bytes.append(tile)
 
         def load_h(g, pieces):
-            t = work_tile([P, GROUP_TILES, D], BF16, "h_raw")
-            step = GROUP_TILES // pieces
-            for k in range(0, GROUP_TILES, step):
-                c0 = g * GROUP_TILES + k
-                nc.sync.dma_start(out=t[:, k : k + step, :], in_=h_view[:, c0 : c0 + step, :])
-            h_raw[g] = t
+            tile = work_tile([P, GROUP_COLS, D], BF16, "h_raw")
+            step = GROUP_COLS // pieces
+            for k in range(0, GROUP_COLS, step):
+                c = g * GROUP_COLS + k
+                nc.sync.dma_start(out=tile[:, k : k + step, :], in_=h_view[:, c : c + step, :])
+            h_raw.append(tile)
 
         def load_w_head(m):
-            t = work_tile([P, PACK, V], BF16, "wh_raw")
-            nc.sync.dma_start(out=t[:], in_=w_head[m].rearrange("(p j) v -> p j v", j=PACK))
-            wh_raw.append(t)
+            tile = work_tile([P, PACK, V], BF16, "w_head_raw")
+            nc.sync.dma_start(out=tile[:], in_=w_head[m].rearrange("(p t) v -> p t v", t=PACK))
+            w_head_raw.append(tile)
 
         w_scale = const.tile([P, PACK], F32)
         nc.scalar.dma_start(out=w_scale[:], in_=w_res_scale.rearrange("o (p t) u -> p (o t u)", t=PACK))
@@ -88,8 +102,8 @@ def tile_medusatypicalacceptanceheads_t_kernel(
         nc.scalar.dma_start(out=a_raw[:], in_=a_skip.rearrange("m (p t) -> p m t", t=PACK))
         g_raw = const.tile([P, HEADS, PACK], BF16)
         nc.scalar.dma_start(out=g_raw[:], in_=g_silu.rearrange("m (p t) -> p m t", t=PACK))
-        temp_raw = const.tile([P, TILES_PER_HEAD], BF16)
-        nc.scalar.dma_start(out=temp_raw[:], in_=temp.rearrange("(p c) -> p c", c=TILES_PER_HEAD))
+        temp_raw = const.tile([P, TOKEN_COLS], BF16)
+        nc.scalar.dma_start(out=temp_raw[:], in_=temp.rearrange("(p c) -> p c", c=TOKEN_COLS))
         load_w_bytes(1)
         load_h(1, 1)
         load_h(2, 1)
@@ -105,387 +119,344 @@ def tile_medusatypicalacceptanceheads_t_kernel(
         nc.scalar.activation(out=warm[:], in_=zero[:], func=ACT.Silu)
         ident = const.tile([P, P], F32)
         make_identity(nc, ident[:])
-        ident_bf = const.tile([P, P], BF16)
-        nc.vector.tensor_copy(out=ident_bf[:], in_=ident[:])
+        ident_bf16 = const.tile([P, P], BF16)
+        nc.vector.tensor_copy(out=ident_bf16[:], in_=ident[:])
 
-        wq, wq_s, whq, whq_s = [], [], [], []
-        w_wide, w_grp = {}, {}
+        w_wide, w_grouped, w_mx = {}, {}, []
 
-        def widen(m, slots, on_scalar):
-            if m not in w_wide:
-                w_wide[m] = work_tile([P, PACK, D], BF16, "w_wide")
-            for t in slots:
-                src = w_bytes[m][:, t, :].bitcast(FP8)
-                if on_scalar:
-                    nc.scalar.activation(out=w_wide[m][:, t, :], in_=src, func=ACT.Copy, scale=w_scale[:, t : t + 1])
+        def widen_w(m):
+            w_wide[m] = work_tile([P, PACK, D], BF16, "w_wide")
+            w_grouped[m] = work_tile([P, PACK, P, PACK], BF16, "w_grouped")
+            for t in range(PACK):
+                byte_values = w_bytes[m][:, t, :].bitcast(FP8)
+                scale = w_scale[:, t : t + 1]
+                if t < PACK // 2:
+                    nc.scalar.activation(out=w_wide[m][:, t, :], in_=byte_values, func=ACT.Copy, scale=scale)
                 else:
                     nc.vector.tensor_scalar(
-                        out=w_wide[m][:, t, :], in0=src, scalar1=w_scale[:, t : t + 1], scalar2=None, op0=ALU.mult
+                        out=w_wide[m][:, t, :], in0=byte_values, scalar1=scale, scalar2=None, op0=ALU.mult
                     )
 
         def group_w(m, lo, hi, copy):
-            if m not in w_grp:
-                w_grp[m] = work_tile([P, PACK, P, PACK], BF16, "w_grp")
             copy(
-                out=w_grp[m][:, lo:hi, :, :],
-                in_=w_wide[m][:].rearrange("p j (m t) -> p t m j", t=PACK)[:, lo:hi, :, :],
+                out=w_grouped[m][:, lo:hi, :, :],
+                in_=w_wide[m][:].rearrange("p j (q t) -> p t q j", t=PACK)[:, lo:hi, :, :],
             )
 
         def quantize_w(m):
-            q = const.tile([P, D], U32, name="w_codes%d" % m, align_bytes=64)
-            s = const.tile([P, D], U8, name="w_scales%d" % m, align_bytes=64)
-            nc.vector.quantize_mx(
-                out=q[:].bitcast(FP8X4), scales=s[:], in_=w_grp[m][:].rearrange("p t m j -> p (t m j)")
-            )
-            wq.append(q)
-            wq_s.append(s)
+            w_mx.append(quantize(const, "w%d" % m, w_grouped[m][:].rearrange("p t q j -> p (t q j)")))
 
-        wh_grp = {}
+        w_head_grouped, w_head_mx = {}, []
 
         def group_w_head(m):
-            t = work_tile([P, V, PACK], BF16, "wh_grp")
+            tile = work_tile([P, V, PACK], BF16, "w_head_grouped")
             nc.vector.tensor_copy(
-                out=t[:].rearrange("p (c i) j -> p c j i", i=4), in_=wh_raw[m][:].rearrange("p j (c i) -> p c j i", i=4)
+                out=tile[:].rearrange("p (c i) t -> p c t i", i=4),
+                in_=w_head_raw[m][:].rearrange("p t (c i) -> p c t i", i=4),
             )
-            wh_grp[m] = t
+            w_head_grouped[m] = tile
 
         def quantize_w_head(m):
-            q = const.tile([P, V], U32, name="wh_codes%d" % m, align_bytes=64)
-            s = const.tile([P, V], U8, name="wh_scales%d" % m, align_bytes=64)
-            nc.vector.quantize_mx(
-                out=q[:].bitcast(FP8X4), scales=s[:], in_=wh_grp[m][:].rearrange("p v j -> p (v j)")
-            )
-            whq.append(q)
-            whq_s.append(s)
+            w_head_mx.append(quantize(const, "w_head%d" % m, w_head_grouped[m][:].rearrange("p v t -> p (v t)")))
 
-        h_t, h_q, h_s, x_banks = {}, {}, {}, {}
+        h_t, h_mx, h_banks, skip_last = {}, {}, {}, {}
 
-        def transpose_h(g, b):
-            xt = psum_x.tile([P, 2, 2, P], F32, name="xt")
+        def transpose_h(g, half):
+            bank = psum_t.tile([P, 2, 2, P], F32, name="h_bank")
             for c in range(2):
-                words = h_raw[g][:, 2 * b + c, :].bitcast(F32)
+                words = h_raw[g][:, 2 * half + c, :].bitcast(F32)
                 for u in range(2):
-                    nc.tensor.transpose(xt[:, c, u, :], words[:, u : D // 2 : 2], ident[:])
-            x_banks[g, b] = xt
+                    nc.tensor.transpose(bank[:, c, u, :], words[:, u : D // 2 : 2], ident[:])
+            h_banks[g, half] = bank
 
-        def empty_h(g, b, copy):
-            if g not in h_t:
+        def empty_h(g, half, copy):
+            if half == 0:
                 h_t[g] = work_tile([P, GROUP, PACK], BF16, "h_t")
-            words = h_t[g][:].rearrange("p n j -> p (n j)").bitcast(F32)
+            words = h_t[g][:].rearrange("p n t -> p (n t)").bitcast(F32)
             copy(
-                out=words[:, GROUP * b : GROUP * (b + 1)].rearrange("p (c r u) -> p c r u", c=2, u=2),
-                in_=x_banks[g, b][:].rearrange("p c u r -> p c r u"),
+                out=words[:, GROUP * half : GROUP * (half + 1)].rearrange("p (c r u) -> p c r u", c=2, u=2),
+                in_=h_banks[g, half][:].rearrange("p c u r -> p c r u"),
             )
 
         def quantize_h(g):
-            q = hq_pool.tile([P, GROUP], U32, name="h_codes", align_bytes=64)
-            s = hq_pool.tile([P, GROUP], U8, name="h_scales", align_bytes=64)
-            nc.vector.quantize_mx(
-                out=q[:].bitcast(FP8X4), scales=s[:], in_=h_t[g][:].rearrange("p n j -> p (n j)")
-            )
-            h_q[g], h_s[g] = q, s
+            h_mx[g] = quantize(h_mx_pool, "h", h_t[g][:].rearrange("p n t -> p (n t)"))
 
-        skip3 = {}
-
-        def skip_last(i):
+        def skip_on_vector(i):
             g, m = divmod(i, HEADS)
-            t = side.tile([P, GROUP], F32, name="skip")
+            skip_last[i] = skip_pool.tile([P, GROUP], F32, name="skip")
             col = m * PACK + PACK - 1
-            if m == SKIP_M:
-                nc.scalar.activation(
-                    out=t[:], in_=h_t[g][:, :, PACK - 1], func=ACT.Copy, scale=a32[:, col : col + 1]
-                )
-            else:
-                nc.vector.tensor_scalar(
-                    out=t[:], in0=h_t[g][:, :, PACK - 1], scalar1=a32[:, col : col + 1], scalar2=None, op0=ALU.mult
-                )
-            skip3[i] = t
+            nc.vector.tensor_scalar(
+                out=skip_last[i][:], in0=h_t[g][:, :, PACK - 1], scalar1=a_cols[:, col : col + 1],
+                scalar2=None, op0=ALU.mult,
+            )
 
-        widen(0, (0, 1), True)
-        widen(0, (2, 3), False)
+        u_banks, s_pairs, r_slots, r_grouped, r_mx = {}, {}, {}, {}, {}
+
+        def project(k):
+            i, t = divmod(k, PACK)
+            if i < UNITS:
+                g, m = divmod(i, HEADS)
+                u_banks[k] = psum_u.tile([P, GROUP], F32, name="u_bank")
+                matmul_mx(u_banks[k], w_mx[m], slice(t * P, (t + 1) * P), h_mx[g])
+
+        def make_r(i, t):
+            g, m = divmod(i, HEADS)
+            k = i * PACK + t
+            col = m * PACK + t
+            if t < TENSOR_SLOTS:
+                skip = psum_s.tile([P, GROUP], F32, name="s_bank")
+                nc.tensor.matmul(skip[:], diag[:, m, t, :], h_t[g][:, :, t], start=True, stop=True)
+            else:
+                skip = skip_last[i]
+            project(k + PROJECT_AHEAD)
+            if t % 2 == 0:
+                s_pairs[i] = work_tile([P, 2, GROUP], F32, "s_pair")
+            silu = s_pairs[i][:, t % 2, :]
+            nc.scalar.activation(out=silu, in_=u_banks[k][:], func=ACT.Silu)
+            if t == 0:
+                r_slots[i] = work_tile([P, PACK, GROUP], BF16, "r_slots")
+            nc.vector.scalar_tensor_tensor(
+                out=r_slots[i][:, t, :], in0=silu, scalar=g_cols[:, col : col + 1], in1=skip[:],
+                op0=ALU.mult, op1=ALU.add,
+            )
+
+        def interleave_on_gpsimd(i):
+            r_grouped[i] = work_tile([P, GROUP, PACK], BF16, "r_grouped")
+            nc.gpsimd.tensor_scalar(
+                out=r_grouped[i][:, :GPSIMD_COLS, :],
+                in0=r_slots[i][:, :, :GPSIMD_COLS].rearrange("p t n -> p n t"),
+                scalar1=1.0, scalar2=0.0, op0=ALU.mult, op1=ALU.add,
+            )
+
+        def interleave_on_scalar(i):
+            nc.scalar.copy(
+                out=r_grouped[i][:, GPSIMD_COLS:, :].rearrange("p (c i) t -> p c t i", i=4),
+                in_=r_slots[i][:, :, GPSIMD_COLS:].rearrange("p t (c i) -> p c t i", i=4),
+            )
+
+        def quantize_r(i):
+            r_mx[i] = quantize(r_mx_pool, "r", r_grouped[i][:].rearrange("p n t -> p (n t)"))
+
+        y_max = const.tile([P, TILES], F32)
+        neg_max = const.tile([P, TILES], F32)
+        sum_w2 = const.tile([P, TILES], F32)
+        weighted_sum = const.tile([P, TILES], F32)
+        eps_arm = const.tile([P, TILES], F32)
+        delta_arm = const.tile([P, TILES], F32)
+        bound = const.tile([P, TILES], F32)
+        base_e = const.tile([P, GROUP_COLS], F32)
+        y_pairs, w_pairs, squares, inv_sum, mean = {}, {}, {}, {}, {}
+        out_view = [out[m].rearrange("(p c) v -> p c v", c=TOKEN_COLS) for m in range(HEADS)]
+
+        def head_of(j):
+            return j // GROUP_COLS % HEADS
+
+        def token_col(j):
+            i, c = divmod(j, GROUP_COLS)
+            return i // HEADS * GROUP_COLS + c
+
+        def stats(i):
+            return slice(i * GROUP_COLS, (i + 1) * GROUP_COLS)
+
+        def logits(j):
+            i, c = divmod(j, GROUP_COLS)
+            col = token_col(j)
+            if j % 2 == 0:
+                bank = psum_u.tile([P, V], F32, name="u_bank")
+                y_pairs[j // 2] = work_tile([P, 2, V], F32, "y_pair")
+            else:
+                bank = psum_s.tile([P, V], F32, name="s_bank")
+            matmul_mx(bank, r_mx[i], slice(c * P, (c + 1) * P), w_head_mx[head_of(j)])
+            nc.vector.tensor_scalar(
+                out=y_pairs[j // 2][:, j % 2, :], in0=bank[:], scalar1=half_inv_temp[:, col : col + 1],
+                scalar2=None, op0=ALU.mult, op1=ALU.max, accum_out=y_max[:, j : j + 1],
+            )
+
+        def negate_max(i):
+            nc.scalar.mul(neg_max[:, stats(i)], y_max[:, stats(i)], -1.0)
+
+        def exponential(j):
+            if j % 2 == 0:
+                w_pairs[j // 2] = work_tile([P, 2, V], F32, "w_pair")
+            nc.scalar.activation(
+                out=w_pairs[j // 2][:, j % 2, :], in_=y_pairs[j // 2][:, j % 2, :], func=ACT.Exp,
+                bias=neg_max[:, j : j + 1],
+            )
+
+        def square(j):
+            squares[j] = square_pool.tile([P, V], F32, name="square")
+            nc.scalar.activation(
+                out=squares[j][:], in_=w_pairs[j // 2][:, j % 2, :], func=ACT.Square,
+                accum_out=sum_w2[:, j : j + 1],
+            )
+
+        def entropy_sum(j):
+            nc.vector.scalar_tensor_tensor(
+                out=squares[j][:], in0=y_pairs[j // 2][:, j % 2, :], scalar=y_max[:, j : j + 1], in1=squares[j][:],
+                op0=ALU.subtract, op1=ALU.mult, accum_out=weighted_sum[:, j : j + 1],
+            )
+
+        def invert_sum(i):
+            inv_sum[i] = stat_pool.tile([P, GROUP_COLS], F32, name="inv_sum")
+            nc.vector.reciprocal(out=inv_sum[i][:], in_=sum_w2[:, stats(i)])
+
+        def take_mean(i):
+            mean[i] = stat_pool.tile([P, GROUP_COLS], F32, name="mean")
+            nc.vector.tensor_tensor(
+                out=mean[i][:], in0=weighted_sum[:, stats(i)], in1=inv_sum[i][:], op=ALU.mult
+            )
+
+        def make_delta_arm(i):
+            if i < UNITS - 1:
+                nc.scalar.activation(out=delta_arm[:, stats(i)], in_=mean[i][:], func=ACT.Exp)
+            else:
+                nc.gpsimd.tensor_tensor(out=delta_arm[:, stats(i)], in0=base_e[:], in1=mean[i][:], op=ALU.pow)
+
+        def make_bound(i):
+            nc.vector.scalar_tensor_tensor(
+                out=bound[:, stats(i)], in0=delta_arm[:, stats(i)], scalar=math.sqrt(DELTA),
+                in1=eps_arm[:, stats(i)], op0=ALU.mult, op1=ALU.min,
+            )
+
+        def logarithm(j):
+            w = w_pairs[j // 2][:, j % 2, :]
+            nc.scalar.activation(out=w, in_=w, func=ACT.Ln, bias=bound[:, j : j + 1])
+
+        def finish(j):
+            y = y_pairs[j // 2][:, j % 2, :]
+            nc.vector.scalar_tensor_tensor(
+                out=y, in0=y, scalar=y_max[:, j : j + 1], in1=w_pairs[j // 2][:, j % 2, :],
+                op0=ALU.subtract, op1=ALU.subtract,
+            )
+            alone = j >= TILES - 2
+            if alone or j % 2 == 1:
+                lo = j % 2 if alone else 0
+                hi = j % 2 + 1
+                col = token_col(j - j % 2)
+                nc.sync.dma_start(
+                    out=out_view[head_of(j)][:, col + lo : col + hi, :], in_=y_pairs[j // 2][:, lo:hi, :]
+                )
+
+        widen_w(0)
         transpose_h(0, 0)
         transpose_h(0, 1)
         group_w(0, 0, 2, nc.vector.tensor_copy)
         group_w(0, 2, 4, nc.scalar.copy)
         empty_h(0, 0, nc.vector.tensor_copy)
         empty_h(0, 1, nc.scalar.copy)
-        a32 = const.tile([P, HEADS * PACK], F32)
-        nc.vector.tensor_copy(out=a32[:], in_=a_raw[:].rearrange("p m t -> p (m t)"))
-        g32 = const.tile([P, HEADS * PACK], F32)
-        nc.vector.tensor_copy(out=g32[:], in_=g_raw[:].rearrange("p m t -> p (m t)"))
+        a_cols = const.tile([P, HEADS * PACK], F32)
+        nc.vector.tensor_copy(out=a_cols[:], in_=a_raw[:].rearrange("p m t -> p (m t)"))
+        g_cols = const.tile([P, HEADS * PACK], F32)
+        nc.vector.tensor_copy(out=g_cols[:], in_=g_raw[:].rearrange("p m t -> p (m t)"))
         quantize_w(0)
         quantize_h(0)
-        skip_last(0)
-        diag = const.tile([P, HEADS, PE_SLOTS, P], BF16)
+        skip_on_vector(0)
+        diag = const.tile([P, HEADS, TENSOR_SLOTS, P], BF16)
 
         def make_diag(m):
-            for t in range(PE_SLOTS):
+            for t in range(TENSOR_SLOTS):
                 col = m * PACK + t
                 nc.vector.tensor_scalar(
-                    out=diag[:, m, t, :], in0=ident_bf[:], scalar1=a32[:, col : col + 1], scalar2=None, op0=ALU.mult
+                    out=diag[:, m, t, :], in0=ident_bf16[:], scalar1=a_cols[:, col : col + 1], scalar2=None,
+                    op0=ALU.mult,
                 )
 
         make_diag(0)
-        widen(1, (0, 1), True)
-        widen(1, (2, 3), False)
+        widen_w(1)
         make_diag(1)
         group_w(1, 0, 4, nc.vector.tensor_copy)
-        two_temp = const.tile([P, TILES_PER_HEAD], F32)
+        two_temp = const.tile([P, TOKEN_COLS], F32)
         nc.vector.tensor_scalar(out=two_temp[:], in0=temp_raw[:], scalar1=2.0, scalar2=None, op0=ALU.mult)
         quantize_w(1)
-        inv2t = const.tile([P, TILES_PER_HEAD], F32)
-        nc.vector.reciprocal(out=inv2t[:], in_=two_temp[:])
+        half_inv_temp = const.tile([P, TOKEN_COLS], F32)
+        nc.vector.reciprocal(out=half_inv_temp[:], in_=two_temp[:])
+        nc.vector.memset(base_e[:], 0.0)
+        nc.gpsimd.tensor_scalar(
+            out=base_e[:], in0=base_e[:], scalar1=0.0, scalar2=math.e, op0=ALU.mult, op1=ALU.add
+        )
 
-        r_cols, r_grp, r_q, r_s = {}, {}, {}, {}
-        s_pair = {}
-
-        u_bank = {}
-
-        def project(k):
-            if k >= UNITS * PACK:
-                return
-            i, t = divmod(k, PACK)
-            g, m = divmod(i, HEADS)
-            u = psum_u.tile([P, GROUP], F32, name="u_bank")
-            nc.tensor.matmul_mx(
-                out=u[:],
-                lhsT=wq[m][:, t * P : (t + 1) * P].bitcast(FP8X4),
-                lhsT_scale=wq_s[m][:, t * P : (t + 1) * P],
-                rhs=h_q[g][:].bitcast(FP8X4),
-                rhs_scale=h_s[g][:],
-                start=True,
-                stop=True,
-            )
-            u_bank[k] = u
-
-        def stage1(i, t):
-            g, m = divmod(i, HEADS)
-            k = i * PACK + t
-            col = m * PACK + t
-            project(k + AHEAD)
-            if t < PE_SLOTS:
-                skip = psum_s.tile([P, GROUP], F32, name="s_bank")
-                nc.tensor.matmul(skip[:], diag[:, m, t, :], h_t[g][:, :, t], start=True, stop=True)
-            else:
-                skip = skip3[i]
-            if t % 2 == 0:
-                s_pair[i] = work_tile([P, 2, GROUP], F32, "s_pair")
-            s = s_pair[i][:, t % 2, :]
-            nc.scalar.activation(out=s, in_=u_bank[k][:], func=ACT.Silu)
-            if t == 0:
-                r_cols[i] = work_tile([P, PACK, GROUP], BF16, "r_cols")
-            nc.vector.scalar_tensor_tensor(
-                out=r_cols[i][:, t, :], in0=s, scalar=g32[:, col : col + 1], in1=skip[:], op0=ALU.mult, op1=ALU.add
-            )
-
-        def inter(i, lo, hi, eng):
-            if hi <= lo:
-                return
-            if i not in r_grp:
-                r_grp[i] = work_tile([P, GROUP, PACK], BF16, "r_grp")
-            if eng == 2:
-                dst = r_grp[i][:, lo:hi, :]
-                src = r_cols[i][:, :, lo:hi].rearrange("p t n -> p n t")
-            else:
-                dst = r_grp[i][:, lo:hi, :].rearrange("p (c i) t -> p c t i", i=4)
-                src = r_cols[i][:, :, lo:hi].rearrange("p t (c i) -> p c t i", i=4)
-            if eng == 0:
-                nc.vector.tensor_copy(out=dst, in_=src)
-            elif eng == 1:
-                nc.scalar.copy(out=dst, in_=src)
-            else:
-                nc.gpsimd.tensor_scalar(
-                    out=dst, in0=src, scalar1=1.0, scalar2=0.0, op0=ALU.mult, op1=ALU.add
-                )
-
-        def quantize_r(i):
-            q = rq_pool.tile([P, GROUP], U32, name="r_codes", align_bytes=64)
-            s = rq_pool.tile([P, GROUP], U8, name="r_scales", align_bytes=64)
-            nc.vector.quantize_mx(
-                out=q[:].bitcast(FP8X4), scales=s[:], in_=r_grp[i][:].rearrange("p n j -> p (n j)")
-            )
-            r_q[i], r_s[i] = q, s
-
-        m2 = const.tile([P, TILES], F32)
-        nm2 = const.tile([P, TILES], F32)
-        sums = const.tile([P, TILES], F32)
-        ents = const.tile([P, TILES], F32)
-        dd = const.tile([P, TILES], F32)
-        y_pair, w_pair, e_tile = {}, {}, {}
-
-        def logits(j):
-            i, c = divmod(j, GROUP_TILES)
-            g, m = divmod(i, HEADS)
-            if j % 2 == 0:
-                z = psum_u.tile([P, V], F32, name="u_bank")
-            else:
-                z = psum_s.tile([P, V], F32, name="s_bank")
-            nc.tensor.matmul_mx(
-                out=z[:],
-                lhsT=r_q[i][:, c * P : (c + 1) * P].bitcast(FP8X4),
-                lhsT_scale=r_s[i][:, c * P : (c + 1) * P],
-                rhs=whq[m][:].bitcast(FP8X4),
-                rhs_scale=whq_s[m][:],
-                start=True,
-                stop=True,
-            )
-            if j % 2 == 0:
-                y_pair[j // 2] = work_tile([P, 2, V], F32, "y_pair")
-            col = g * GROUP_TILES + c
-            nc.vector.tensor_scalar(
-                out=y_pair[j // 2][:, j % 2, :], in0=z[:], scalar1=inv2t[:, col : col + 1], scalar2=None,
-                op0=ALU.mult, op1=ALU.max, accum_out=m2[:, j : j + 1],
-            )
-
-        def expo(j):
-            if j % GROUP_TILES == 0:
-                nc.scalar.mul(nm2[:, j : j + GROUP_TILES], m2[:, j : j + GROUP_TILES], -1.0)
-            if j % 2 == 0:
-                w_pair[j // 2] = work_tile([P, 2, V], F32, "w_pair")
-            nc.scalar.activation(
-                out=w_pair[j // 2][:, j % 2, :], in_=y_pair[j // 2][:, j % 2, :], func=ACT.Exp,
-                bias=nm2[:, j : j + 1],
-            )
-
-        def squares(j):
-            e_tile[j] = e_pool.tile([P, V], F32, name="e")
-            nc.scalar.activation(
-                out=e_tile[j][:], in_=w_pair[j // 2][:, j % 2, :], func=ACT.Square, accum_out=sums[:, j : j + 1]
-            )
-
-        def weighted(j):
-            e = e_tile[j]
-            nc.vector.scalar_tensor_tensor(
-                out=e[:], in0=y_pair[j // 2][:, j % 2, :], scalar=m2[:, j : j + 1], in1=e[:],
-                op0=ALU.subtract, op1=ALU.mult, accum_out=ents[:, j : j + 1],
-            )
-
-        st = {}
-
-        def unit(i):
-            return slice(i * GROUP_TILES, (i + 1) * GROUP_TILES)
-
-        arm = const.tile([P, TILES], F32)
-        root = const.tile([P, TILES], F32)
-
-        def thr_a(i):
-            st[i, "r"] = stat.tile([P, GROUP_TILES], F32, name="rec")
-            nc.vector.reciprocal(out=st[i, "r"][:], in_=sums[:, unit(i)])
-
-        def thr_b(i):
-            st[i, "q"] = stat.tile([P, GROUP_TILES], F32, name="q")
-            nc.vector.tensor_tensor(out=st[i, "q"][:], in0=ents[:, unit(i)], in1=st[i, "r"][:], op=ALU.mult)
-
-        def thr_c(i):
-            nc.scalar.activation(out=arm[:, unit(i)], in_=st[i, "q"][:], func=ACT.Exp)
-
-        def thr_d(lo, hi):
-            nc.scalar.activation(out=root[:, lo:hi], in_=sums[:, lo:hi], func=ACT.Sqrt, scale=EPS)
-            nc.vector.scalar_tensor_tensor(
-                out=dd[:, lo:hi], in0=arm[:, lo:hi], scalar=math.sqrt(DELTA), in1=root[:, lo:hi],
-                op0=ALU.mult, op1=ALU.min,
-            )
-
-        def lnp(j):
-            w = w_pair[j // 2][:, j % 2, :]
-            nc.scalar.activation(out=w, in_=w, func=ACT.Ln, bias=dd[:, j : j + 1])
-
-        def final(j):
-            y = y_pair[j // 2][:, j % 2, :]
-            nc.vector.scalar_tensor_tensor(
-                out=y, in0=y, scalar=m2[:, j : j + 1], in1=w_pair[j // 2][:, j % 2, :],
-                op0=ALU.subtract, op1=ALU.subtract,
-            )
-            if j % 2 == 1:
-                i, c = divmod(j - 1, GROUP_TILES)
-                g, m = divmod(i, HEADS)
-                c0 = g * GROUP_TILES + c
-                nc.sync.dma_start(
-                    out=out[m].rearrange("(p c) v -> p c v", c=TILES_PER_HEAD)[:, c0 : c0 + 2, :],
-                    in_=y_pair[j // 2][:],
-                )
-
-        done = 0
-        for k in range(AHEAD):
+        issued = 0
+        for k in range(PROJECT_AHEAD):
             project(k)
         for i in range(UNITS):
             g, m = divmod(i, HEADS)
-            nxt = g + 1 < GROUPS
-            if m == 0 and nxt:
+            fetch = m == 0 and g + 1 < GROUPS
+            if fetch:
                 transpose_h(g + 1, 0)
-            if m == 0 and nxt:
                 transpose_h(g + 1, 1)
-            stage1(i, 0)
+            make_r(i, 0)
             if i > 0:
-                inter(i - 1, INTER_V, INTER_G, 2)
-            if m == 0 and nxt:
+                interleave_on_gpsimd(i - 1)
+            if fetch:
                 empty_h(g + 1, 0, nc.scalar.copy)
-            stage1(i, 1)
-            if m == 0 and nxt:
+            make_r(i, 1)
+            if fetch:
                 empty_h(g + 1, 1, nc.scalar.copy)
-            stage1(i, 2)
-            if i > 0:
-                inter(i - 1, 0, INTER_V, 0)
-            if i > 0:
-                inter(i - 1, INTER_G, GROUP, 1)
+            make_r(i, 2)
             if i + 1 < UNITS:
-                skip_last(i + 1)
-            if m == 0 and nxt:
+                skip_on_vector(i + 1)
+            if fetch:
                 quantize_h(g + 1)
-            if i in (2, 4):
-                group_w_head(i // 2 - 1)
-            if i in (5, 7):
-                quantize_w_head((i - 5) // 2)
-            if PRE.get(i, 0) > 1:
-                logits(done)
-                done += 1
+            for head in range(HEADS):
+                if i == 2 + 2 * head:
+                    group_w_head(head)
+                if i == 5 + 2 * head:
+                    quantize_w_head(head)
             if i > 1:
                 quantize_r(i - 2)
-            stage1(i, 3)
-            if PRE.get(i, 0) > 0:
-                logits(done)
-                done += 1
-
+            make_r(i, 3)
+            if i > 0:
+                interleave_on_scalar(i - 1)
+            if i >= UNITS - EARLY_UNITS:
+                logits(issued)
+                issued += 1
         last = UNITS - 1
-        inter(last, 0, INTER_V, 0)
-        inter(last, INTER_V, INTER_G, 2)
-        inter(last, INTER_G, GROUP, 1)
+        interleave_on_gpsimd(last)
+        interleave_on_scalar(last)
         quantize_r(last - 1)
-        logits(done)
-        logits(done + 1)
-        done += 2
+        for f in range(EARLY_LAST):
+            logits(issued)
+            issued += 1
         quantize_r(last)
+        negate_max(0)
+
         j = 0
-        for start, end in CHUNKS:
+        for start, end in SWEEPS:
             while j < end + LAG + 2:
-                while done < min(j + LOOK + 1, end + LAG + 4, TILES):
-                    logits(done)
-                    done += 1
-                k = j - LAG - 2
-                if k >= 0 and k % GROUP_TILES == 3:
-                    thr_c(k // GROUP_TILES)
+                behind = j - LAG
+                if 0 <= behind < TILES:
+                    if behind % GROUP_COLS == GROUP_COLS - 1:
+                        invert_sum(behind // GROUP_COLS)
+                    entropy_sum(behind)
+                if behind > 0 and behind % GROUP_COLS == 0:
+                    take_mean(behind // GROUP_COLS - 1)
+                while issued < min(j + LOOK + 1, end + LAG + GROUP_COLS, TILES):
+                    logits(issued)
+                    issued += 1
+                if behind > 1 and behind % GROUP_COLS == 1:
+                    make_delta_arm(behind // GROUP_COLS - 1)
                 if j < TILES:
-                    expo(j)
+                    exponential(j)
+                if j + 1 < TILES and (j + 1) % GROUP_COLS == 0:
+                    negate_max((j + 1) // GROUP_COLS)
                 if 0 < j <= TILES:
-                    squares(j - 1)
-                k = j - LAG - 1
-                if k >= 0 and k % GROUP_TILES == 3:
-                    thr_b(k // GROUP_TILES)
-                k = j - LAG
-                if 0 <= k < TILES:
-                    weighted(k)
-                    if k % GROUP_TILES == 3:
-                        thr_a(k // GROUP_TILES)
+                    square(j - 1)
                 j += 1
+            nc.scalar.activation(out=eps_arm[:, start:end], in_=sum_w2[:, start:end], func=ACT.Sqrt, scale=EPS)
+            first_unit, end_unit = start // GROUP_COLS, end // GROUP_COLS
             if end < TILES:
-                for f in range(X1):
-                    logits(done)
-                    done += 1
-            thr_d(start, end)
+                for f in range(BRIDGE_BEFORE):
+                    logits(issued)
+                    issued += 1
+            make_bound(first_unit)
+            make_bound(first_unit + 1)
             if end < TILES:
-                for f in range(X2):
-                    logits(done)
-                    done += 1
+                for f in range(BRIDGE_AFTER):
+                    logits(issued)
+                    issued += 1
             for f in range(start, end):
-                lnp(f)
-                final(f)
+                ahead = f // GROUP_COLS + 2
+                if f % GROUP_COLS == 0 and ahead < end_unit:
+                    make_bound(ahead)
+                logarithm(f)
+                finish(f)

import math
from contextlib import ExitStack

import concourse.mybir as mybir
from concourse.masks import make_identity

HEADS, TOKENS, D, V = 2, 4096, 512, 512
EPS, DELTA = 0.001, 0.3
FLOPS = 2 * HEADS * TOKENS * D * (D + V)

P = 128
PACK = 4
TOKEN_COLS = TOKENS // P
GROUP_COLS = 4
GROUP = GROUP_COLS * P
GROUPS = TOKENS // GROUP
UNITS = GROUPS * HEADS
TILES = UNITS * GROUP_COLS

TENSOR_SLOTS = 3
GPSIMD_COLS = 256
PROJECT_AHEAD = 2
SWEEPS = ((0, 24), (24, 64))
WORK_BUFS = 40
LOOK, LAG = 5, 4
EARLY_UNITS, EARLY_LAST = 4, 2
BRIDGE_BEFORE, BRIDGE_AFTER = 3, 3

F32 = mybir.dt.float32
BF16 = mybir.dt.bfloat16
U32 = mybir.dt.uint32
U8 = mybir.dt.uint8
FP8 = mybir.dt.float8_e4m3fn
FP8X4 = mybir.dt.float8_e4m3fn_x4
ALU = mybir.AluOpType
ACT = mybir.ActivationFunctionType


def tile_medusatypicalacceptanceheads_t_kernel(
    tc, h, w_res_bytes, w_res_scale, a_skip, g_silu, w_head, temp, out
):
    nc = tc.nc
    with ExitStack() as ctx:
        const = ctx.enter_context(tc.tile_pool(name="const", bufs=1))
        work = ctx.enter_context(tc.tile_pool(name="work", bufs=WORK_BUFS))
        h_mx_pool = ctx.enter_context(tc.tile_pool(name="h_mx_pool", bufs=2))
        r_mx_pool = ctx.enter_context(tc.tile_pool(name="r_mx_pool", bufs=UNITS))
        skip_pool = ctx.enter_context(tc.tile_pool(name="skip_pool", bufs=2))
        square_pool = ctx.enter_context(tc.tile_pool(name="square_pool", bufs=LAG + 1))
        stat_pool = ctx.enter_context(tc.tile_pool(name="stat_pool", bufs=4))
        psum_t = ctx.enter_context(tc.psum_pool(name="psum_t", bufs=2))
        psum_u = ctx.enter_context(tc.psum_pool(name="psum_u", bufs=3))
        psum_s = ctx.enter_context(tc.psum_pool(name="psum_s", bufs=3))
        ctx.enter_context(tc.manual_schedule())

        def work_tile(shape, dtype, name):
            return work.tile(shape, dtype, name=name, tag="work", align_bytes=64)

        def quantize(pool, name, grouped):
            codes = pool.tile([P, 512], U32, name=name + "_codes", align_bytes=64)
            scales = pool.tile([P, 512], U8, name=name + "_scales", align_bytes=64)
            nc.vector.quantize_mx(out=codes[:].bitcast(FP8X4), scales=scales[:], in_=grouped)
            return codes, scales

        def matmul_mx(bank, stationary, cols, moving):
            nc.tensor.matmul_mx(
                out=bank[:],
                lhsT=stationary[0][:, cols].bitcast(FP8X4),
                lhsT_scale=stationary[1][:, cols],
                rhs=moving[0][:].bitcast(FP8X4),
                rhs_scale=moving[1][:],
                start=True,
                stop=True,
            )

        h_view = h.rearrange("(p c) d -> p c d", c=TOKEN_COLS)
        w_bytes, h_raw, w_head_raw = [], [], []

        def load_w_bytes(m):
            tile = const.tile([P, PACK, D], U8, name="w_bytes%d" % m)
            nc.sync.dma_start(out=tile[:], in_=w_res_bytes[m].rearrange("(p t) n -> p t n", t=PACK))
            w_bytes.append(tile)

        def load_h(g, pieces):
            tile = work_tile([P, GROUP_COLS, D], BF16, "h_raw")
            step = GROUP_COLS // pieces
            for k in range(0, GROUP_COLS, step):
                c = g * GROUP_COLS + k
                nc.sync.dma_start(out=tile[:, k : k + step, :], in_=h_view[:, c : c + step, :])
            h_raw.append(tile)

        def load_w_head(m):
            tile = work_tile([P, PACK, V], BF16, "w_head_raw")
            nc.sync.dma_start(out=tile[:], in_=w_head[m].rearrange("(p t) v -> p t v", t=PACK))
            w_head_raw.append(tile)

        w_scale = const.tile([P, PACK], F32)
        nc.scalar.dma_start(out=w_scale[:], in_=w_res_scale.rearrange("o (p t) u -> p (o t u)", t=PACK))
        load_w_bytes(0)
        load_h(0, 2)
        a_raw = const.tile([P, HEADS, PACK], BF16)
        nc.scalar.dma_start(out=a_raw[:], in_=a_skip.rearrange("m (p t) -> p m t", t=PACK))
        g_raw = const.tile([P, HEADS, PACK], BF16)
        nc.scalar.dma_start(out=g_raw[:], in_=g_silu.rearrange("m (p t) -> p m t", t=PACK))
        temp_raw = const.tile([P, TOKEN_COLS], BF16)
        nc.scalar.dma_start(out=temp_raw[:], in_=temp.rearrange("(p c) -> p c", c=TOKEN_COLS))
        load_w_bytes(1)
        load_h(1, 1)
        load_h(2, 1)
        load_w_head(0)
        load_h(3, 1)
        load_w_head(1)
        for g in range(4, GROUPS):
            load_h(g, 1)

        zero = const.tile([P, 1], F32)
        nc.vector.memset(zero[:], 0.0)
        warm = const.tile([P, 1], F32)
        nc.scalar.activation(out=warm[:], in_=zero[:], func=ACT.Silu)
        ident = const.tile([P, P], F32)
        make_identity(nc, ident[:])
        ident_bf16 = const.tile([P, P], BF16)
        nc.vector.tensor_copy(out=ident_bf16[:], in_=ident[:])

        w_wide, w_grouped, w_mx = {}, {}, []

        def widen_w(m):
            w_wide[m] = work_tile([P, PACK, D], BF16, "w_wide")
            w_grouped[m] = work_tile([P, PACK, P, PACK], BF16, "w_grouped")
            for t in range(PACK):
                byte_values = w_bytes[m][:, t, :].bitcast(FP8)
                scale = w_scale[:, t : t + 1]
                if t < PACK // 2:
                    nc.scalar.activation(out=w_wide[m][:, t, :], in_=byte_values, func=ACT.Copy, scale=scale)
                else:
                    nc.vector.tensor_scalar(
                        out=w_wide[m][:, t, :], in0=byte_values, scalar1=scale, scalar2=None, op0=ALU.mult
                    )

        def group_w(m, lo, hi, copy):
            copy(
                out=w_grouped[m][:, lo:hi, :, :],
                in_=w_wide[m][:].rearrange("p j (q t) -> p t q j", t=PACK)[:, lo:hi, :, :],
            )

        def quantize_w(m):
            w_mx.append(quantize(const, "w%d" % m, w_grouped[m][:].rearrange("p t q j -> p (t q j)")))

        w_head_grouped, w_head_mx = {}, []

        def group_w_head(m):
            tile = work_tile([P, V, PACK], BF16, "w_head_grouped")
            nc.vector.tensor_copy(
                out=tile[:].rearrange("p (c i) t -> p c t i", i=4),
                in_=w_head_raw[m][:].rearrange("p t (c i) -> p c t i", i=4),
            )
            w_head_grouped[m] = tile

        def quantize_w_head(m):
            w_head_mx.append(quantize(const, "w_head%d" % m, w_head_grouped[m][:].rearrange("p v t -> p (v t)")))

        h_t, h_mx, h_banks, skip_last = {}, {}, {}, {}

        def transpose_h(g, half):
            bank = psum_t.tile([P, 2, 2, P], F32, name="h_bank")
            for c in range(2):
                words = h_raw[g][:, 2 * half + c, :].bitcast(F32)
                for u in range(2):
                    nc.tensor.transpose(bank[:, c, u, :], words[:, u : D // 2 : 2], ident[:])
            h_banks[g, half] = bank

        def empty_h(g, half, copy):
            if half == 0:
                h_t[g] = work_tile([P, GROUP, PACK], BF16, "h_t")
            words = h_t[g][:].rearrange("p n t -> p (n t)").bitcast(F32)
            copy(
                out=words[:, GROUP * half : GROUP * (half + 1)].rearrange("p (c r u) -> p c r u", c=2, u=2),
                in_=h_banks[g, half][:].rearrange("p c u r -> p c r u"),
            )

        def quantize_h(g):
            h_mx[g] = quantize(h_mx_pool, "h", h_t[g][:].rearrange("p n t -> p (n t)"))

        def skip_on_vector(i):
            g, m = divmod(i, HEADS)
            skip_last[i] = skip_pool.tile([P, GROUP], F32, name="skip")
            col = m * PACK + PACK - 1
            nc.vector.tensor_scalar(
                out=skip_last[i][:], in0=h_t[g][:, :, PACK - 1], scalar1=a_cols[:, col : col + 1],
                scalar2=None, op0=ALU.mult,
            )

        u_banks, s_pairs, r_slots, r_grouped, r_mx = {}, {}, {}, {}, {}

        def project(k):
            i, t = divmod(k, PACK)
            if i < UNITS:
                g, m = divmod(i, HEADS)
                u_banks[k] = psum_u.tile([P, GROUP], F32, name="u_bank")
                matmul_mx(u_banks[k], w_mx[m], slice(t * P, (t + 1) * P), h_mx[g])

        def make_r(i, t):
            g, m = divmod(i, HEADS)
            k = i * PACK + t
            col = m * PACK + t
            if t < TENSOR_SLOTS:
                skip = psum_s.tile([P, GROUP], F32, name="s_bank")
                nc.tensor.matmul(skip[:], diag[:, m, t, :], h_t[g][:, :, t], start=True, stop=True)
            else:
                skip = skip_last[i]
            project(k + PROJECT_AHEAD)
            if t % 2 == 0:
                s_pairs[i] = work_tile([P, 2, GROUP], F32, "s_pair")
            silu = s_pairs[i][:, t % 2, :]
            nc.scalar.activation(out=silu, in_=u_banks[k][:], func=ACT.Silu)
            if t == 0:
                r_slots[i] = work_tile([P, PACK, GROUP], BF16, "r_slots")
            nc.vector.scalar_tensor_tensor(
                out=r_slots[i][:, t, :], in0=silu, scalar=g_cols[:, col : col + 1], in1=skip[:],
                op0=ALU.mult, op1=ALU.add,
            )

        def interleave_on_gpsimd(i):
            r_grouped[i] = work_tile([P, GROUP, PACK], BF16, "r_grouped")
            nc.gpsimd.tensor_scalar(
                out=r_grouped[i][:, :GPSIMD_COLS, :],
                in0=r_slots[i][:, :, :GPSIMD_COLS].rearrange("p t n -> p n t"),
                scalar1=1.0, scalar2=0.0, op0=ALU.mult, op1=ALU.add,
            )

        def interleave_on_scalar(i):
            nc.scalar.copy(
                out=r_grouped[i][:, GPSIMD_COLS:, :].rearrange("p (c i) t -> p c t i", i=4),
                in_=r_slots[i][:, :, GPSIMD_COLS:].rearrange("p t (c i) -> p c t i", i=4),
            )

        def quantize_r(i):
            r_mx[i] = quantize(r_mx_pool, "r", r_grouped[i][:].rearrange("p n t -> p (n t)"))

        y_max = const.tile([P, TILES], F32)
        neg_max = const.tile([P, TILES], F32)
        sum_w2 = const.tile([P, TILES], F32)
        weighted_sum = const.tile([P, TILES], F32)
        eps_arm = const.tile([P, TILES], F32)
        delta_arm = const.tile([P, TILES], F32)
        bound = const.tile([P, TILES], F32)
        base_e = const.tile([P, GROUP_COLS], F32)
        y_pairs, w_pairs, squares, inv_sum, mean = {}, {}, {}, {}, {}
        out_view = [out[m].rearrange("(p c) v -> p c v", c=TOKEN_COLS) for m in range(HEADS)]

        def head_of(j):
            return j // GROUP_COLS % HEADS

        def token_col(j):
            i, c = divmod(j, GROUP_COLS)
            return i // HEADS * GROUP_COLS + c

        def stats(i):
            return slice(i * GROUP_COLS, (i + 1) * GROUP_COLS)

        def logits(j):
            i, c = divmod(j, GROUP_COLS)
            col = token_col(j)
            if j % 2 == 0:
                bank = psum_u.tile([P, V], F32, name="u_bank")
                y_pairs[j // 2] = work_tile([P, 2, V], F32, "y_pair")
            else:
                bank = psum_s.tile([P, V], F32, name="s_bank")
            matmul_mx(bank, r_mx[i], slice(c * P, (c + 1) * P), w_head_mx[head_of(j)])
            nc.vector.tensor_scalar(
                out=y_pairs[j // 2][:, j % 2, :], in0=bank[:], scalar1=half_inv_temp[:, col : col + 1],
                scalar2=None, op0=ALU.mult, op1=ALU.max, accum_out=y_max[:, j : j + 1],
            )

        def negate_max(i):
            nc.scalar.mul(neg_max[:, stats(i)], y_max[:, stats(i)], -1.0)

        def exponential(j):
            if j % 2 == 0:
                w_pairs[j // 2] = work_tile([P, 2, V], F32, "w_pair")
            nc.scalar.activation(
                out=w_pairs[j // 2][:, j % 2, :], in_=y_pairs[j // 2][:, j % 2, :], func=ACT.Exp,
                bias=neg_max[:, j : j + 1],
            )

        def square(j):
            squares[j] = square_pool.tile([P, V], F32, name="square")
            nc.scalar.activation(
                out=squares[j][:], in_=w_pairs[j // 2][:, j % 2, :], func=ACT.Square,
                accum_out=sum_w2[:, j : j + 1],
            )

        def entropy_sum(j):
            nc.vector.scalar_tensor_tensor(
                out=squares[j][:], in0=y_pairs[j // 2][:, j % 2, :], scalar=y_max[:, j : j + 1], in1=squares[j][:],
                op0=ALU.subtract, op1=ALU.mult, accum_out=weighted_sum[:, j : j + 1],
            )

        def invert_sum(i):
            inv_sum[i] = stat_pool.tile([P, GROUP_COLS], F32, name="inv_sum")
            nc.vector.reciprocal(out=inv_sum[i][:], in_=sum_w2[:, stats(i)])

        def take_mean(i):
            mean[i] = stat_pool.tile([P, GROUP_COLS], F32, name="mean")
            nc.vector.tensor_tensor(
                out=mean[i][:], in0=weighted_sum[:, stats(i)], in1=inv_sum[i][:], op=ALU.mult
            )

        def make_delta_arm(i):
            if i < UNITS - 1:
                nc.scalar.activation(out=delta_arm[:, stats(i)], in_=mean[i][:], func=ACT.Exp)
            else:
                nc.gpsimd.tensor_tensor(out=delta_arm[:, stats(i)], in0=base_e[:], in1=mean[i][:], op=ALU.pow)

        def make_bound(i):
            nc.vector.scalar_tensor_tensor(
                out=bound[:, stats(i)], in0=delta_arm[:, stats(i)], scalar=math.sqrt(DELTA),
                in1=eps_arm[:, stats(i)], op0=ALU.mult, op1=ALU.min,
            )

        def logarithm(j):
            w = w_pairs[j // 2][:, j % 2, :]
            nc.scalar.activation(out=w, in_=w, func=ACT.Ln, bias=bound[:, j : j + 1])

        def finish(j):
            y = y_pairs[j // 2][:, j % 2, :]
            nc.vector.scalar_tensor_tensor(
                out=y, in0=y, scalar=y_max[:, j : j + 1], in1=w_pairs[j // 2][:, j % 2, :],
                op0=ALU.subtract, op1=ALU.subtract,
            )
            alone = j >= TILES - 2
            if alone or j % 2 == 1:
                lo = j % 2 if alone else 0
                hi = j % 2 + 1
                col = token_col(j - j % 2)
                nc.sync.dma_start(
                    out=out_view[head_of(j)][:, col + lo : col + hi, :], in_=y_pairs[j // 2][:, lo:hi, :]
                )

        widen_w(0)
        transpose_h(0, 0)
        transpose_h(0, 1)
        group_w(0, 0, 2, nc.vector.tensor_copy)
        group_w(0, 2, 4, nc.scalar.copy)
        empty_h(0, 0, nc.vector.tensor_copy)
        empty_h(0, 1, nc.scalar.copy)
        a_cols = const.tile([P, HEADS * PACK], F32)
        nc.vector.tensor_copy(out=a_cols[:], in_=a_raw[:].rearrange("p m t -> p (m t)"))
        g_cols = const.tile([P, HEADS * PACK], F32)
        nc.vector.tensor_copy(out=g_cols[:], in_=g_raw[:].rearrange("p m t -> p (m t)"))
        quantize_w(0)
        quantize_h(0)
        skip_on_vector(0)
        diag = const.tile([P, HEADS, TENSOR_SLOTS, P], BF16)

        def make_diag(m):
            for t in range(TENSOR_SLOTS):
                col = m * PACK + t
                nc.vector.tensor_scalar(
                    out=diag[:, m, t, :], in0=ident_bf16[:], scalar1=a_cols[:, col : col + 1], scalar2=None,
                    op0=ALU.mult,
                )

        make_diag(0)
        widen_w(1)
        make_diag(1)
        group_w(1, 0, 4, nc.vector.tensor_copy)
        two_temp = const.tile([P, TOKEN_COLS], F32)
        nc.vector.tensor_scalar(out=two_temp[:], in0=temp_raw[:], scalar1=2.0, scalar2=None, op0=ALU.mult)
        quantize_w(1)
        half_inv_temp = const.tile([P, TOKEN_COLS], F32)
        nc.vector.reciprocal(out=half_inv_temp[:], in_=two_temp[:])
        nc.vector.memset(base_e[:], 0.0)
        nc.gpsimd.tensor_scalar(
            out=base_e[:], in0=base_e[:], scalar1=0.0, scalar2=math.e, op0=ALU.mult, op1=ALU.add
        )

        issued = 0
        for k in range(PROJECT_AHEAD):
            project(k)
        for i in range(UNITS):
            g, m = divmod(i, HEADS)
            fetch = m == 0 and g + 1 < GROUPS
            if fetch:
                transpose_h(g + 1, 0)
                transpose_h(g + 1, 1)
            make_r(i, 0)
            if i > 0:
                interleave_on_gpsimd(i - 1)
            if fetch:
                empty_h(g + 1, 0, nc.scalar.copy)
            make_r(i, 1)
            if fetch:
                empty_h(g + 1, 1, nc.scalar.copy)
            make_r(i, 2)
            if i + 1 < UNITS:
                skip_on_vector(i + 1)
            if fetch:
                quantize_h(g + 1)
            for head in range(HEADS):
                if i == 2 + 2 * head:
                    group_w_head(head)
                if i == 5 + 2 * head:
                    quantize_w_head(head)
            if i > 1:
                quantize_r(i - 2)
            make_r(i, 3)
            if i > 0:
                interleave_on_scalar(i - 1)
            if i >= UNITS - EARLY_UNITS:
                logits(issued)
                issued += 1
        last = UNITS - 1
        interleave_on_gpsimd(last)
        interleave_on_scalar(last)
        quantize_r(last - 1)
        for f in range(EARLY_LAST):
            logits(issued)
            issued += 1
        quantize_r(last)
        negate_max(0)

        j = 0
        for start, end in SWEEPS:
            while j < end + LAG + 2:
                behind = j - LAG
                if 0 <= behind < TILES:
                    if behind % GROUP_COLS == GROUP_COLS - 1:
                        invert_sum(behind // GROUP_COLS)
                    entropy_sum(behind)
                if behind > 0 and behind % GROUP_COLS == 0:
                    take_mean(behind // GROUP_COLS - 1)
                while issued < min(j + LOOK + 1, end + LAG + GROUP_COLS, TILES):
                    logits(issued)
                    issued += 1
                if behind > 1 and behind % GROUP_COLS == 1:
                    make_delta_arm(behind // GROUP_COLS - 1)
                if j < TILES:
                    exponential(j)
                if j + 1 < TILES and (j + 1) % GROUP_COLS == 0:
                    negate_max((j + 1) // GROUP_COLS)
                if 0 < j <= TILES:
                    square(j - 1)
                j += 1
            nc.scalar.activation(out=eps_arm[:, start:end], in_=sum_w2[:, start:end], func=ACT.Sqrt, scale=EPS)
            first_unit, end_unit = start // GROUP_COLS, end // GROUP_COLS
            if end < TILES:
                for f in range(BRIDGE_BEFORE):
                    logits(issued)
                    issued += 1
            make_bound(first_unit)
            make_bound(first_unit + 1)
            if end < TILES:
                for f in range(BRIDGE_AFTER):
                    logits(issued)
                    issued += 1
            for f in range(start, end):
                ahead = f // GROUP_COLS + 2
                if f % GROUP_COLS == 0 and ahead < end_unit:
                    make_bound(ahead)
                logarithm(f)
                finish(f)
